import numpy as np, ml_dtypes
CORES = [5,29,101,125,133,157,229,253]
N = 8
import mx_ref
BF = ml_dtypes.bfloat16
def gcols(t, e):
    v = np.concatenate([t.reshape(8, 16, -1, 4), np.zeros((8, 16, 1, 4), BF)], axis=2)
    return np.ascontiguousarray(np.stack([v[g][:, e[g]] for g in range(8)])).reshape(128, -1)
def tile(rs):
    return np.stack(rs, axis=2).reshape(128, -1).astype(BF)
def pick(q, e):
    c = np.concatenate([q[0].reshape(128, -1, 4), np.zeros((128, 1, 4), np.uint8)], axis=1); s = np.concatenate([q[1], np.ones((16, 1), np.uint8)], axis=1)
    return (np.ascontiguousarray(c[:, e].reshape(128, -1)), np.ascontiguousarray(s[:, e]))
def join(*qs):
    return (np.concatenate([q[0] for q in qs], axis=1), np.concatenate([q[1] for q in qs], axis=1))
def put(q, e, v):
    c, s = q[0].reshape(128, -1, 4).copy(), q[1].copy(); c[:, e] = v[0].reshape(128, -1, 4); s[:, e] = v[1]
    return (c.reshape(128, -1), s)
def pk(c, s):
    return (np.ascontiguousarray(c), mx_ref.live(s))
def emit(q):
    return q[0], q[1]
def packed(v, rng):
    q = [mx_ref.quantize(np.ascontiguousarray(v[r])) for r in range(N)]
    return np.stack([a for a, b in q]), np.stack([mx_ref.plane(b, rng) for a, b in q])
def values_of_codes():
    e, c = np.zeros((128, 128, 4), np.float32), np.zeros((128, 2, 4), np.uint8)
    e[np.arange(128), np.arange(128), 0] = 1
    c[:127, :, 0] = np.arange(256).reshape(2, 128).T[:127]
    return mx_ref.matmul(mx_ref.quantize(e.reshape(128, 512).astype(BF)), (c.reshape(128, 8), np.full((16, 2), 127, np.uint8))).T.reshape(-1).astype(np.float64)
CODE_VALUE, SCALE_VALUE = values_of_codes(), 2.0 ** (np.arange(256) - 127.0)
def decode(q):
    return (CODE_VALUE[q[0]].reshape(16, 8, -1, 4) * SCALE_VALUE[q[1]][:, None, :, None] + 0.0).reshape(128, -1).astype(np.float32)
def f(rng, *shape):
    return mx_ref.flush((rng.standard_normal(shape, dtype=np.float32) * np.exp2(rng.integers(-2, 3, shape[:-1] + (1,)))).astype(BF))
def wide(rng, *shape, cols=0):
    v = rng.standard_normal(shape, dtype=np.float32) * np.exp2(rng.integers(-12, 13, shape)).astype(np.float32)
    if cols: v *= np.repeat(np.exp2(rng.integers(-cols, cols + 1, shape[:-2] + (1, shape[-1] // 4))) * (rng.random(shape[:-2] + (1, shape[-1] // 4)) > 0.0625), 4, axis=-1).astype(np.float32)
    return mx_ref.flush(v.astype(BF))
C, K, LB = 192, 48, 6
def layer(w, g, t):
    return tile([mx_ref.matmul(pick(w, np.arange(128 * b, 128 * b + 128)), g) * np.float32(0.015625) + t[:, b::4] for b in range(4)])
def numbers_of(rng):
    return {"x": np.array(f(rng, N, 128, 4 * C)), "q": np.array(f(rng, N, 128, 4 * K)), "u": np.array(f(rng, N, 128, 512)), "z": np.array(f(rng, N, 128, 512)), "v": np.array(f(rng, N, 128, 512))}
def weights(rng, w):
    c, p = packed(w, rng)
    return {"wc": c, "ws": p}
def still(rng, k):
    w = np.zeros((N, 128, 4, 128, 4), np.float32)
    i = np.arange(128)
    for b in range(4): w[:, i, b, i, b] = k
    return weights(rng, w.reshape(N, 128, 2048).astype(BF))
def marked(rng, s, size):
    d = numbers_of(rng)
    c = size[:, None, None, None, None]
    m = rng.choice([-1.0, 0.0, 1.0], (N, 8, 8, C, 4))
    m[:, :, :4, :, 0] = 1.125 * s
    m[:, :, 4:, :, 0] = s
    m[..., 3] = 0
    d["x"].reshape(N, 8, 16, C, 4)[:, :, :8] = (m * c).astype(np.float32).astype(BF)
    h = rng.choice([1.0, 1.0, -1.0, 0.0], (N, 8, LB + 7, K))
    h[..., 0] = -1
    h[..., 1] = 1
    h[:, :, :LB, 2] = 1
    h[:, :, LB:, 2] = -1
    h[:, :, :LB, 3] = -1
    h[:, :, LB:, 3] = 1
    h[..., 4] = 0
    m = rng.choice([-1.0, 0.0, 1.0], (N, 8, 16, K, 4))
    m[:, :, :LB + 7, :, 3] = 1.125 * h
    m[..., 0][:, :, (np.arange(LB + 7) + 8) % 16] = h
    d["q"] = (m * c).astype(np.float32).astype(BF).reshape(N, 128, 4 * K)
    u, z = d["u"].reshape(N, 8, 16, 128, 4), d["z"].reshape(N, 8, 16, 128, 4)
    u[:, :, :, ::16] = 0
    z[:, :, :, np.arange(128) % 16 < LB + 7] = 0
    i = np.arange(N)
    plus, minus = (1.125 * size).astype(np.float32).astype(BF), (-1.25 * size).astype(np.float32).astype(BF)
    for g in range(8):
        u[i, g, i % 4, 16 * g, 0] = plus
        u[i, g, 4 + i % 4, 16 * g, 0] = minus
        for e in range(LB + 7):
            z[i, g, e, 16 * g + e, 3] = plus
            z[i, g, (e + 8) % 16, 16 * g + e, 0] = minus
    return d
def setup_inputs(rng):
    return {**numbers_of(rng), **weights(rng, f(rng, N, 128, 2048))}
def setup_inputs_near(rng):
    size = np.where(rng.permutation(N) < N // 2, 2.0 ** -30, 1.0)
    s = rng.choice([1.0, 1.0, -1.0, 0.0], (N, 8, 4, C))
    a, i = (1 << LB) - 1, np.arange(N)
    s[..., a] = -1
    s[i, :, i % 4, a] = 1
    s[..., a + 126] = -1
    s[..., a + 127] = 1
    return {**marked(rng, s, size), **still(rng, 64)}
def setup_inputs_flat(rng):
    s = np.zeros((N, 8, 4, C))
    for r in range(N):
        for i in range(4):
            k = rng.permutation(8) % 6
            for g in range(8):
                a = s[r, g, i]
                if k[g] == 5: a[:] = rng.choice([1.0, -1.0, 0.0], C)
                elif k[g] != 2:
                    a[:] = 1.0 if k[g] in (0, 4) else -1.0
                    if k[g] > 2: a[int(rng.integers(C))] *= -1.0
    d = marked(rng, s, np.ones(N))
    d["x"][int(rng.integers(N))] = 0
    return {**d, **still(rng, 64)}
def setup_inputs_huge(rng):
    d = numbers_of(rng)
    h = (np.arange(N) + int(rng.integers(4))) % 4
    c = rng.choice([-1.0, 1.0], (N, 8, C))
    c[:, :, 0] = 1
    c[:, :, 1] = -1
    c[h == 0] = c[h == 0][:, :1]
    c[h > 1] = 1
    x = 2.0 ** 30 * (0.65 + 0.1 * rng.random((N, 8, 16, C, 4))) * c[:, :, None, :, None]
    k = rng.choice([-1.0, 1.0], (N, 128, K, 4))
    k[:, :, ::2] = rng.choice([-1.0, 1.0], (N, 1, K // 2, 1))
    q = 2.0 ** 29 * (0.75 + 0.25 * rng.random((N, 128, K, 4))) * k
    s = rng.choice([-1.0, 1.0], (N, 8))
    s[h == 0] = -np.roll(s, -1, axis=0)[h == 0]
    s = np.maximum(np.eye(8), (h == 0)[:, None, None]) * s[:, None, :]
    u = d["u"].reshape(N, 8, 16, 128, 4)
    u[:, :, :, ::16] = (2.0 ** 30 * (0.9 + 0.1 * rng.random((N, 8, 16, 8, 4))) * s[:, :, None, :, None] + 0.0).astype(np.float32).astype(BF)
    z = 2.0 ** 30 * (0.75 + 0.25 * rng.random((N, 128, 128, 4))) * rng.choice([-1.0, 1.0], (N, 1, 128, 1))
    d["x"] = x.astype(np.float32).astype(BF).reshape(N, 128, 4 * C)
    d["q"] = q.astype(np.float32).astype(BF).reshape(N, 128, 4 * K)
    d["z"] = z.astype(np.float32).astype(BF).reshape(N, 128, 512)
    return {**d, **still(rng, 1)}
def setup_inputs_spread(rng):
    d = setup_inputs(rng)
    d["x"] = wide(rng, N, 128, 4 * C, cols=6)
    d["q"] = wide(rng, N, 128, 4 * K, cols=6)
    return d
def check_inputs(d):
    b = []
    for k in ("x", "q", "u", "z", "v"):
        a = np.abs(d[k].astype(np.float32))
        if not (np.isfinite(a).all() and ((a == 0) | (a >= 2.0 ** -30) & (a <= 2.0 ** 30)).all()): b.append("a value of " + k)
    return b
def reference(x, q, u, z, v, wc, ws):
    qu = [mx_ref.quantize(u[r]) for r in range(N)]
    lay = [pk(wc[r], ws[r]) for r in range(N)]
    y, ol = np.zeros((N, 128, K), np.float32), np.zeros((N, 8, K), np.float32)
    oc, osc = np.zeros((N, 128, 4 * K), np.uint8), np.zeros((N, 16, K), np.uint8)
    weight = (1 << np.arange(7))[:, None]
    for r in range(N):
        t, at, key = x[r], np.tile(np.arange(C), (8, 1)), np.zeros((8, C), np.int64)
        level, path = [], []
        for l in range(3):
            h = (r + l) % N
            if l:
                g = mx_ref.quantize(gcols(t, o))
                t = layer(lay[h], g, decode(g))
                at = np.take_along_axis(np.argsort(o, axis=1), at, axis=1)
            bit = mx_ref.matmul(qu[h], mx_ref.quantize(t))[::16] > 0
            o = np.argsort(bit, axis=1, kind="stable")
            key = 2 * key + np.take_along_axis(bit, at, axis=1)
            level.append(t)
            path.append(at)
        e = mx_ref.matmul(mx_ref.quantize(z[r]), mx_ref.quantize(q[r])).reshape(8, 16, K) > 0
        lo = np.sum(e[:, :LB] * weight[:LB], axis=1)
        k = np.sum(e[:, LB:LB + 7] * weight, axis=1)
        i = np.argsort(key[np.arange(8)[:, None, None], lo[:, :, None] + np.arange(128)], axis=2, kind="stable")
        a = lo + np.take_along_axis(i, k[:, :, None], axis=2)[:, :, 0]
        part = [gcols(level[l], np.take_along_axis(path[l], a, axis=1)) for l in range(3)]
        first = ((decode(mx_ref.quantize(part[2])) + decode(mx_ref.quantize(part[1]))) * np.float32(0.5)).astype(BF)
        both = ((decode(mx_ref.quantize(first)) + part[0].astype(np.float32)) * np.float32(0.5)).astype(BF)
        last = mx_ref.quantize(layer(lay[r], mx_ref.quantize(both), q[r].astype(np.float32)))
        y[r] = mx_ref.matmul(mx_ref.quantize(v[r]), last)
        ol[r] = a
        oc[r], osc[r] = emit(last)
    return {"y": y, "ol": ol, "oc": oc, "osc": osc}

@@ -1,0 +1,472 @@
+from concourse.bass import DstId, RemoteDMATransfer
+from concourse.mybir import dt, AluOpType, ActivationFunctionType
+
+C, K = 192, 48
+BF, F32, I32, U16, U8, X4 = "bfloat16", "float32", "int32", "uint16", "uint8", "float8_e4m3fn_x4"
+SCRATCH = {"ps": ("psum", [128, 4096], F32)}
+for _d, _names in (
+        (X4, "wq:512 uq:128 urq:128 zq:128 vq:128 qq:128 qrq:384 eq:512 hq:512 f0q:384 f1q:384 b1q:320 bq:128 xq:128 "
+             "l1q:192 l2q:192 l3q:176 r1q:64 r2q:64"),
+        (U8, "wp:512 up:128 urp:128 zp:128 vp:128 qp:128 qrp:384 ep:512 hp:512 f0p:384 f1p:384 b1p:320 bp:128 xp:128 "
+             "l1p:192 l2p:192 l3p:320 r1p:256 r2p:256"),
+        (BF, "xt:768 ut:512 zt:512 vt:512 qt:512 f0:768 t1:768 f1:768 t2:768 hs:1536 b1:512 bt:512 xo:512 gt:768 a0:192 "
+             "et:2048 zero:512 idn:128 ir:192 ip:192 jv:192 neg:192 one:16 m3:576 m4:192 c16:96 c16a:96 hm:48 "
+             "i0:580 i1:580 ex3:576 ex4:192 o0:192 o1:192 eb:384 eg:48 yg:96 nb:192 ya:194 yb:192 junk:576 "
+             "cm:582 rr:582 us:582 o4:768 c4:768"),
+        (F32, "xf:192 q64:192 yt:48 olt:48 olx:48 old:4 cf:8 cs:32 idf:128 eh:48 s0:12 s1:12 ye:96 "
+              "u0:12 u1:12 u2:12 u3:12 uc:4 sm:24"),
+        (I32, "ci:48 cj:8"),
+        (U16, "offu:8 offq:24 offe:4 p0:12 p1:12 g0:48 g1:48 so:6 m1:18 m2:12 j2:4 j4:12 "
+              "lm1:18 lm2:12 lo1:48 lj:4 rm1:18 rm2:12 ro1:48")):
+    for _e in _names.split():
+        SCRATCH[_e.split(":")[0]] = ("sbuf", [128, int(_e.split(":")[1])], _d)
+SEMAPHORES = ["nV", "nA", "nP", "nG", "dx", "du", "dq", "dz", "dv", "dwq", "dwp", "st", "ls",
+              "a1", "a2", "a3", "am1", "am2", "ao", "aj", "h1", "h2", "hm1", "hm2", "ho"]
+ALU, ACT = AluOpType, ActivationFunctionType
+
+
+def _mask(engines):
+    m = 0
+    for e in engines:
+        m |= 1 << e
+    return m
+
+
+def _helpers(topo, src, dst):
+    h = [c for c in topo.cores_of(src) if c != src and topo.may_write(c, dst)]
+    return sorted(h, key=lambda c: (topo.die(c) != topo.die(src), c))
+
+
+def _hand_on(g, core, T, topo):
+    n = len(T.cores)
+    mine = [r for r in range(n) if T.cores[r] in topo.cores_of(core)]
+    if not mine:
+        return
+    src, nxt, prv = T.cores[mine[0]], T.cores[(mine[0] + 1) % n], T.cores[(mine[0] - 1) % n]
+    hs = _helpers(topo, src, nxt)
+    if core not in hs:
+        return
+    i = hs.index(core)
+    full = len(topo.engines(src, core))
+    sent = [0]
+
+    def on(wait, cnt, out, in_, sem, dst):
+        g.wait_ge(T.sem[wait], cnt)
+        rid, pid = topo.addr(dst, core)
+        g.remote_dma(out, in_, T.sem[sem], T.sem.ls, pid, rid, topo.mask(core, dst))
+        sent[0] += len(topo.engines(core, dst))
+
+    def tile(s):
+        if i < 3:
+            on("h" + s, full // len(hs), T["l%sq" % s][:, 64 * i:64 * i + 64].bitcast(dt.uint8),
+               T["r%sq" % s][:].bitcast(dt.uint8), "a" + s, nxt)
+        else:
+            on("h" + s, full // len(hs), T["l%sp" % s][:], T["r%sp" % s][:, 0:C], "a" + s, nxt)
+
+    tile("1")
+    if i == 0:
+        on("hm1", full, T.lm1[:], T.rm1[:], "am1", nxt)
+    tile("2")
+    if i == 0:
+        on("hm2", full, T.lm2[:], T.rm2[:], "am2", nxt)
+    if core == _helpers(topo, src, prv)[1]:
+        on("ho", full, T.lo1[:], T.ro1[:], "ao", prv)
+    g.wait_ge(T.sem.ls, sent[0])
+
+
+def rank_program(g, core, T, topo):
+    rank = T.rank_of(core)
+    if rank is None:
+        _hand_on(g, core, T, topo)
+        return
+    n = len(T.cores)
+    nxt, prv, prv2, nxt2 = (T.cores[(rank + d) % n] for d in (1, -1, -2, 2))
+    Q = {"V": g.vector, "A": g.scalar, "P": g.tensor, "G": g, "S": g.sync}
+    known = {q: {} for q in Q}
+    clock, acc, count = {}, {}, {}
+
+    def a(name, lo=0, hi=None, step=1):
+        hi = SCRATCH[name][1][1] if hi is None else hi
+        cols = range(lo, hi, step)
+        if name == "ps":
+            cols = range(lo // 512 * 512, lo // 512 * 512 + 512)
+        return (T[name][:, lo:hi:step] if step != 1 else T[name][:, lo:hi], name, frozenset(cols))
+
+    def need(q, tok):
+        s, v = tok
+        if known[q].get(s, 0) >= v:
+            return
+        Q[q].wait_ge(T.sem[s], v)
+        for s2, v2 in clock.get(tok, {}).items():
+            known[q][s2] = max(known[q].get(s2, 0), v2)
+        known[q][s] = v
+
+    def order(q, reads, writes):
+        toks = {}
+        for lst, wr in ((reads, False), (writes, True)):
+            for _, name, cols in lst:
+                for tq, tok, c2, w2 in acc.get(name, []):
+                    if q == "P" and tq == "P":
+                        continue
+                    if (wr or w2 or (name == "ps" and tq != q)) and cols & c2:
+                        toks[tok[0]] = max(toks.get(tok[0], 0), tok[1])
+        for s in sorted(toks, key=lambda s: s == "n" + q):
+            need(q, (s, toks[s]))
+
+    def note(q, tok, reads, writes):
+        clock[tok] = dict(known[q])
+        for lst, wr in ((reads, False), (writes, True)):
+            for _, name, cols in lst:
+                acc.setdefault(name, []).append((q, tok, cols, wr))
+
+    def op(q, fn, reads, writes):
+        order(q, reads, writes)
+        s = "n" + q
+        fn().then_inc(T.sem[s], 1)
+        count[s] = count.get(s, 0) + 1
+        note(q, (s, count[s]), reads, writes)
+
+    def lands(sem, cnt, *writes):
+        count[sem] = cnt
+        note("S", (sem, cnt), [], writes)
+
+    def load(q, sem, out, src, w):
+        Q[q].dma_start(out, src).then_inc(T.sem[sem], 16)
+        count[sem] = 16
+        note(q, (sem, 16), [], [w])
+
+    def store(q, out, src, r):
+        order(q, [r], [])
+        Q[q].dma_start(out, src).then_inc(T.sem.st, 16)
+        count["st"] = count.get("st", 0) + 16
+
+    def send(moves):
+        order("G", [m[5] for m in moves], [])
+        if len(moves) == 1:
+            d, sem, eng, out, in_, _ = moves[0]
+            rid, pid = topo.addr(d, core)
+            g.remote_dma(out, in_, T.sem[sem], T.sem.ls, pid, rid, _mask(eng))
+        else:
+            tr = []
+            for d, sem, eng, out, in_, _ in moves:
+                rid, pid = topo.addr(d, core)
+                tr.append(RemoteDMATransfer(dst_ids=[DstId(rid=rid, pnc=pid)], dma_engine_mask=_mask(eng),
+                                            remote_sem=T.sem[sem], src=in_, dst=out))
+            g.remote_dma_fused(tr, local_sem=T.sem.ls)
+        count["ls"] = count.get("ls", 0) + sum(len(m[2]) for m in moves)
+
+    def sc(x):
+        return (x[0], [x]) if isinstance(x, tuple) else (x, [])
+
+    def ts(out, in0, s1, op0, s2=None, op1=None, off=None):
+        (v1, r1), (v2, r2) = sc(s1), sc(s2)
+        src = in0[0] if off is None else in0[0].indirect(off[0])
+        args = (out[0], src, v1, v2, op0) + (() if op1 is None else (op1,))
+        op("V", lambda: g.vector.tensor_scalar(*args), [in0] + r1 + r2 + ([off] if off else []), [out])
+
+    def tt(out, in0, in1, o):
+        op("V", lambda: g.vector.tensor_tensor(out[0], in0[0], in1[0], o), [in0, in1], [out])
+
+    def scan(out, d0, d1, init, op0, op1):
+        v, r = sc(init)
+        op("V", lambda: g.vector.tensor_tensor_scan(out[0], d0[0], d1[0], v, op0, op1), [d0, d1] + r, [out])
+
+    def fill(out, v):
+        op("V", lambda: g.vector.memset(out[0], v), [], [out])
+
+    def copy(out, in_):
+        op("V", lambda: g.vector.tensor_copy(out[0], in_[0]), [in_], [out])
+
+    def recip(out, in_):
+        op("V", lambda: g.vector.reciprocal(out[0], in_[0]), [in_], [out])
+
+    def gather(q, out, win, off, scale=None):
+        if q == "A":
+            kw = {} if scale is None else {"scale": scale}
+            op("A", lambda: g.scalar.activation(out[0], win[0].indirect(off[0]), ACT.Copy, **kw), [win, off], [out])
+        elif scale is None:
+            op("V", lambda: g.vector.tensor_copy(out[0], win[0].indirect(off[0])), [win, off], [out])
+        else:
+            ts(out, win, scale, ALU.mult, off=off)
+
+    def scaled(q, out, in_, s):
+        if q == "A":
+            op("A", lambda: g.scalar.activation(out[0], in_[0], ACT.Copy, scale=s), [in_], [out])
+        else:
+            ts(out, in_, s, ALU.mult)
+
+    def quant(nm, lo, w, tile):
+        c, p = a(nm + "q", lo, lo + w), a(nm + "p", lo, lo + w)
+        op("V", lambda: g.vector.quantize_mx(c[0], p[0], tile[0]), [tile], [c, p])
+
+    def pick(dst, src, w, off):
+        c, p, c0, p0 = a(dst + "q", 0, w), a(dst + "p", 0, w), a(src + "q"), a(src + "p")
+        op("V", lambda: g.vector.tensor_copy(c[0].bitcast(dt.uint32), c0[0].bitcast(dt.uint32).indirect(off[0])), [c0, off], [c])
+        op("A", lambda: g.scalar.activation(p[0], p0[0].indirect(off[0]), ACT.Copy), [p0, off], [p])
+
+    def mm(bank, st, slo, mv, mlo, w, start=True, stop=True):
+        o = a("ps", 512 * bank, 512 * bank + w)
+        r = [a(st + "q", slo, slo + 128), a(st + "p", slo, slo + 128), a(mv + "q", mlo, mlo + w), a(mv + "p", mlo, mlo + w)]
+        op("P", lambda: g.tensor.matmul_mx(o[0], r[0][0], r[1][0], r[2][0], r[3][0], start, stop), r, [o])
+
+    def bank(b, lo, hi):
+        return a("ps", 512 * b + lo, 512 * b + hi)
+
+    def iota(out, pattern, base, cm, small):
+        kw = {"allow_small_or_imprecise_dtypes": True} if small else {}
+        op("G", lambda: g.iota(out[0], pattern, base, cm, **kw), [], [out])
+
+    hs = _helpers(topo, core, nxt)
+    back = _helpers(topo, core, prv)[1]
+
+    def send_tile(nm, s):
+        eng = topo.engines(core, hs[0])
+        half, moves = len(eng) // 2, []
+        for i, h in enumerate(hs):
+            e = eng[(i % 2) * half + i // 2:(i % 2) * half + half:2]
+            if i < 3:
+                r = a(nm + "q", 64 * i, 64 * i + 64)
+                moves.append((h, "h" + s, e, T["r%sq" % s][:].bitcast(dt.uint8), r[0].bitcast(dt.uint8), r))
+            else:
+                r = a(nm + "p", 0, 256)
+                moves.append((h, "h" + s, e, T["r%sp" % s][:], r[0], r))
+        send(moves)
+
+    def via(src, i):
+        return len(topo.engines(_helpers(topo, src, core)[i], core))
+
+    direct = topo.engines(core, prv2)
+    lands("a1", sum(via(prv, i) for i in range(4)), a("l1q"), a("l1p"))
+    lands("a2", sum(via(prv, i) for i in range(4)), a("l2q"), a("l2p"))
+    lands("a3", len(topo.engines(nxt2, core)), a("l3q", 128, 176), a("l3p", 128, 320))
+    lands("am1", via(prv, 0), a("lm1"))
+    lands("am2", via(prv, 0), a("lm2"))
+    lands("ao", via(nxt, 1), a("lo1"))
+    lands("aj", len(topo.engines(nxt2, core)), a("lj"))
+
+    load("A", "du", T.ut[:], T.u[:], a("ut"))
+    load("S", "dx", T.xt[:], T.x[:], a("xt"))
+    need("S", ("dx", 16))
+    load("S", "dq", T.qt[:, 0:C], T.q[:], a("qt", 0, C))
+    load("S", "dz", T.zt[:], T.z[:], a("zt"))
+    load("S", "dwq", T.wq[:].bitcast(dt.uint8), T.wc[:], a("wq"))
+    load("S", "dwp", T.wp[:], T.ws[:], a("wp"))
+    load("S", "dv", T.vt[:], T.v[:], a("vt"))
+
+    pm, sel, q4, sc3, sc4 = (a("cf", i, i + 1) for i in range(5))
+    iota(a("ci", 0, 1), [[0, 1]], 0, 1, False)
+    iota(a("ci", 8, 16), [[16, 8]], 0, 0, False)
+    iota(a("ir"), [[0, 12], [1, 16]], 0, 0, True)
+    iota(a("ip"), [[0, 48], [1, 4]], 0, 0, True)
+    iota(a("jv"), [[4, C]], 4, 0, True)
+    iota(a("idf"), [[1, 128]], 0, -1, True)
+    iota(a("ci", 16, 20), [[128, 4]], 0, 1, False)
+    iota(a("ci", 24, 48), [[16, 3], [0, 8]], 0, 0, False)
+    fill(a("et", 0, 512), 0.0)
+    fill(a("neg"), -1.0)
+    fill(a("i0", 0, 3), 256.0)
+    fill(a("one"), 1.0)
+    fill(a("o0"), 0.0)
+    for b in range(1, 4):
+        scaled("A", a("et", 512 * b, 512 * b + 512), a("et", 0, 512), 1.0)
+    ts(a("cj", 0, 1), a("ci", 0, 1), 15, ALU.bitwise_and)
+    ts(a("cj", 2, 3), a("ci", 0, 1), 3, ALU.bitwise_and)
+    copy(a("offu"), a("ci", 8, 16))
+    copy(pm, a("cj", 0, 1))
+    ts(a("cj", 1, 2), a("cj", 0, 1), 2, ALU.arith_shift_right)
+    ts(q4, a("cj", 2, 3), -4.0, ALU.add)
+    copy(sel, a("cj", 1, 2))
+    ts(a("m3", 0, 576, 3), a("ir"), pm, ALU.is_gt, 4.0, ALU.mult)
+    ts(a("m3", 1, 576, 3), a("m3", 0, 576, 3), 257.0 / 1024, ALU.mult, -1.0 / 256, ALU.add)
+    scan(a("cs", 0, 16), a("m3", 0, 48, 3), a("neg", 0, 16), 0.0, ALU.mult, ALU.min)
+    ts(a("m3", 2, 576, 3), a("m3", 0, 576, 3), 64.25, ALU.mult, -256.0, ALU.add)
+    ts(a("m4"), a("ip"), sel, ALU.is_gt, 256.0, ALU.mult)
+    recip(sc3, a("cs", 15, 16))
+    scan(a("cs", 16, 20), a("m4", 0, 4), a("one", 0, 4), 0.0, ALU.mult, ALU.max)
+    recip(sc4, a("cs", 19, 20))
+
+    def counts(s, nnb, y, y2, last):
+        ts(nnb, s, 0.0, ALU.is_le, -1.0, ALU.mult)
+        scan(y, nnb, a("neg"), 256.0, ALU.add, ALU.max)
+        scan(y2, a("neg"), nnb, last, ALU.add, ALU.subtract)
+
+    def sort(lv, s, t):
+        i, p, o, gl, f = "i%d" % lv, a("p%d" % lv), a("o%d" % lv), "g%d" % lv, "f%d" % lv
+        counts(s, a(i, 4, 580, 3), a(i, 3, 579, 3), a(i, 5, 580, 3), a(i, 576, 577))
+        scan(a("ex3"), a("m3"), a(i, 3, 579), 0.0, ALU.mult, ALU.max)
+        ts(p, a("ex3", 47, 576, 48), sc3, ALU.mult, 255.0, ALU.add)
+        op("V", lambda: g.vector.tensor_copy(o[0].indirect(p[0]), T.jv[:]), [p, a("jv")], [o])
+        scan(a("ex4"), a("m4"), o, 0.0, ALU.mult, ALU.max)
+        ts(a(gl), a("ex4", 3, C, 4), sc4, ALU.mult, q4, ALU.add)
+        gather("A", a(f, 384, 768), a(t), a(gl, 24, 48))
+        gather("V", a(f, 0, 384), a(t), a(gl, 0, 24))
+        quant(f, 0, C, a(f))
+
+    def step(lv, st, off, msg, wide):
+        i = "i%d" % lv
+        gather("A", a("yg"), a(i, 0, 579), off)
+        ts(a("uc", 3, 4), a(i, 576, 577), -1.0, ALU.mult, 256.0, ALU.add)
+        scan(a("ye"), a("yg"), a("c16"), 0.0, ALU.max, ALU.add)
+        ts(a("u0", 0, 6), a("ye", 15, 96, 16), -1.0, ALU.mult, -768.0, ALU.add)
+        tt(a("u0", 6, 9), a("u0", 0, 3), a(st, 9, 12), ALU.add)
+        tt(a("u1", 0, 6), a(st, 0, 6), a("u0", 0, 6), ALU.subtract)
+        tt(a("u1", 6, 9), a(st, 6, 9), a("u0", 3, 6), ALU.subtract)
+        tt(a("uc", 0, 3), a("u0", 6, 9), a("u0", 3, 6), ALU.is_ge)
+        for s in range(3):
+            ts(a("u2", s, 9, 3), a("u1", s, 9, 3), a("uc", 3, 4), ALU.add, a("uc", s, s + 1), ALU.mult)
+        tt(a("u3", 0, 9), a("u0", 0, 9), a("u2", 0, 9), ALU.max)
+        if wide:
+            ts(a(msg, 0, 6), a("u3", 0, 6), 3.0, ALU.mult)
+        tt(a("u3", 9, 12), a("u3", 6, 9), a("u3", 0, 3), ALU.subtract)
+        copy(a(msg, 6, 18) if wide else a(msg), a("u3"))
+
+    def layer(land, t, nm, lo):
+        for b in range(4):
+            mm(b, "w", 128 * b, land, 0, C, True, False)
+            mm(b, "e", 128 * b, land, 0, C, False, True)
+            scaled("AV"[b % 2], a(t, b, 768, 4), bank(b, 0, C), 0.015625)
+        quant(nm, lo, C, a(t))
+
+    quant("u", 0, 128, a("ut"))
+    pick("ur", "u", 128, a("offu"))
+    quant("f0", C, C, a("xt"))
+    mm(4, "ur", 0, "f0", C, C)
+    sort(0, bank(4, 0, C), "xt")
+    send_tile("f0", "1")
+
+    ts(a("idn"), a("idf"), 0.0, ALU.is_equal)
+    for b in range(4):
+        scaled("A", a("et", 512 * b + b, 512 * b + 512, 4), a("idn"), 64.0)
+    fill(a("qt", C, 512), 0.0)
+    fill(a("i1", 0, 3), 256.0)
+    fill(a("o1"), 0.0)
+    ts(a("offq"), a("ci", 24, 48), pm, ALU.add)
+    copy(a("offe"), a("ci", 16, 20))
+    quant("q", 0, 128, a("qt"))
+    quant("z", 0, 128, a("zt"))
+    quant("e", 0, 512, a("et"))
+    pick("qr", "q", 384, a("offq"))
+    for c in range(3):
+        mm(5 + c, "qr", 128 * c, "z", 0, 128)
+    fill(a("hm"), 0.5)
+    ts(a("c16a"), a("ir", 0, 96), pm, ALU.is_lt, -1024.0, ALU.mult)
+    ts(a("c16"), a("ir", 0, 96), pm, ALU.is_equal, 1024.0, ALU.mult)
+    fill(a("hm", 0, K, 16), 0.0)
+    fill(a("hm", 6, K, 16), 0.0)
+    tt(a("c16"), a("c16"), a("c16a"), ALU.add)
+    for c in range(3):
+        ts(a("eb", 128 * c, 128 * c + 128), bank(5 + c, 0, 128), 0.0, ALU.is_gt)
+    ts(a("c16", 15, 96, 16), a("c16", 15, 96, 16), -2048.0, ALU.add)
+    gather("V", a("eg"), a("eb"), a("offe", 0, 3))
+    scan(a("eh"), a("hm"), a("eg"), 0.0, ALU.mult, ALU.add)
+    ts(a("s0", 0, 3), a("eh", 5, K, 16), 32.0, ALU.mult)
+    ts(a("s0", 3, 6), a("eh", 5, K, 16), 32.0, ALU.mult, 128.0, ALU.add)
+    ts(a("s0", 9, 12), a("eh", 12, K, 16), 64.0, ALU.mult)
+    ts(a("so"), a("s0", 0, 6), 3.0, ALU.mult)
+    tt(a("s0", 6, 9), a("s0", 0, 3), a("s0", 9, 12), ALU.add)
+    step(0, "s0", a("so"), "m1", True)
+    send([(hs[0], "hm1", topo.engines(core, hs[0]), T.rm1[:], T.m1[:], a("m1"))])
+
+    layer("l1", "t1", "f1", C)
+    mm(4, "ur", 0, "f1", C, C)
+    sort(1, bank(4, 0, C), "t1")
+    send_tile("f1", "2")
+    send([(back, "ho", topo.engines(core, back), T.ro1[:], T.g1[:], a("g1"))])
+    copy(a("s1"), a("lm1", 6, 18))
+    step(1, "s1", a("lm1", 0, 6), "m2", False)
+    send([(hs[0], "hm2", topo.engines(core, hs[0]), T.rm2[:], T.m2[:], a("m2"))])
+
+    for b in range(4):
+        scaled("A", a("et", 512 * b + b, 512 * b + 512, 4), a("idn"), 0.5)
+    scaled("A", a("q64"), a("qt", 0, C), 64.0)
+    fill(a("hs"), 0.0)
+    fill(a("ya", 0, 1), 256.0)
+    fill(a("rr"), 1.0)
+    fill(a("cm", 192, 582, 194), 0.0)
+    fill(a("cm", 193, 582, 194), -192.0)
+    fill(a("b1", C, 512), 0.0)
+    fill(a("j2"), 0)
+    fill(a("rr", 0, 582, 194), 0.0)
+    fill(a("rr", 192, 582, 194), 2.0)
+    quant("h", 0, 512, a("et"))
+    fill(a("zero"), 0.0)
+    fill(a("bt", C, 512), 0.0)
+    fill(a("xo", C, 512), 0.0)
+    fill(a("o4"), 0.0)
+    quant("l3", 0, 128, a("zero"))
+    quant("v", 0, 128, a("vt"))
+    ts(a("o4", 0, 768, 4), a("o0"), 0.25, ALU.mult, -1.0, ALU.add)
+
+    def hpart(q, b):
+        scaled(q, a("hs", 384 * b, 384 * b + 384, 2), bank(4 + b, 0, C), 1.0)
+
+    layer("l2", "t2", "b1", 128)
+    for b in range(4):
+        mm(4 + b, "h", 128 * b, "l2", 0, C, True, False)
+    mm(0, "ur", 0, "b1", 128, C)
+    for b in range(4):
+        mm(4 + b, "h", 128 * b, "b1", 128, C, False, True)
+    kf, kc, cb, bias, dd, sums = (a("sm", 4 * i, 4 * i + 3) for i in range(6))
+    copy(kf, a("lm2", 9, 12))
+    ts(kc, a("lm2", 9, 12), -1024.0, ALU.add)
+    hpart("A", 0)
+    counts(bank(0, 0, C), a("nb"), a("ya", 1, 193), a("yb"), a("ya", 192, 193))
+    gather("A", a("yg"), a("ya", 0, 193), a("lm2", 0, 6))
+    hpart("A", 1)
+    ts(cb, a("lm2", 6, 9), 768.5, ALU.add, a("ya", 192, 193), ALU.subtract)
+    hpart("V", 2)
+    scan(a("ye"), a("yg"), a("c16"), 0.0, ALU.max, ALU.add)
+    el, eh = a("ye", 15, 48, 16), a("ye", 63, 96, 16)
+    tt(bias, eh, cb, ALU.add)
+    for s in range(3):
+        o, bc, ac = a("junk", C * s, C * s + C), a("sm", 12 + s, 13 + s), a("sm", 20 + s, 21 + s)
+        op("A", lambda o=o, bc=bc, ac=ac: g.scalar.activation(o[0], T.yb[:], ACT.Sign, bias=bc[0], accum_out=ac[0]),
+           [a("yb"), bc], [o, ac])
+    tt(dd, eh, kf, ALU.add)
+    for s in range(3):
+        ts(a("cm", 194 * s, 194 * s + C), a("ya", 1, 193), a("sm", 4 + s, 5 + s), ALU.add,
+           a("ye", 16 * s + 15, 16 * s + 16), ALU.is_ge)
+        if s == 0:
+            tt(a("rr", 193, 582, 194), dd, el, ALU.is_lt)
+    scan(a("us"), a("rr"), a("cm"), 0.0, ALU.mult, ALU.add)
+    hpart("V", 3)
+    for s in range(3):
+        ts(a("j2", s, s + 1), a("sm", 20 + s, 21 + s), a("us", 194 * s + 193, 194 * s + 194), ALU.max, 192.0, ALU.add)
+    send([(prv2, "aj", direct, T.lj[:], T.j2[:], a("j2"))])
+    for b in range(4):
+        gather("AVAV"[b], a("b1", b, C, 4), a("hs", 384 * b, 384 * b + 384), a("j2", 0, 3))
+    quant("b1", 0, 128, a("b1"))
+    rc, rp = a("b1q", 0, K), a("b1p", 0, C)
+    send([(prv2, "a3", direct[0::2], T.l3q[:, 128:176].bitcast(dt.uint8), rc[0].bitcast(dt.uint8), rc),
+          (prv2, "a3", direct[1::2], T.l3p[:, 128:320], rp[0], rp)])
+
+    gather("A", a("gt", 384, 768), a("f0"), a("lo1", 24, 48))
+    gather("V", a("gt", 0, 384), a("f0"), a("lo1", 0, 24))
+    gather("A", a("c4", 384, 768), a("o4"), a("lo1", 24, 48))
+    gather("V", a("c4", 0, 384), a("o4"), a("lo1", 0, 24))
+    for b in range(4):
+        ts(a("j4", 3 * b, 3 * b + 3), a("lj", 0, 3), 2.0, ALU.mult, float(b), ALU.add)
+    gather("A", a("a0", 96, C), a("gt"), a("j4", 6, 12), 0.5)
+    gather("V", a("a0", 0, 96), a("gt"), a("j4", 0, 6), 0.5)
+    gather("A", a("olt"), a("c4"), a("j4", 0, 3))
+    for c in range(3):
+        scan(a("olx", 16 * c, 16 * c + 16), a("olt", c, K, 3), a("c16", 0, 16), 0.0, ALU.max, ALU.add)
+    ts(a("old", 0, 3), a("olx", 15, K, 16), 1024.0, ALU.add)
+    store("S", T.ol[:], T.old[:, 0:3], a("old", 0, 3))
+    for b in range(4):
+        mm(b, "h", 128 * b, "l3", K, 128)
+        tt(a("bt", b, C, 4), bank(b, 80, 128), a("a0", K * b, K * b + K), ALU.add)
+    quant("b", 0, 128, a("bt"))
+    for b in range(4):
+        mm(4 + b, "w", 128 * b, "b", 0, 128)
+        tt(a("xf", b, C, 4), bank(4 + b, 0, K), a("q64", b, C, 4), ALU.add)
+        scaled("AAAV"[b], a("xo", b, C, 4), a("xf", b, C, 4), 0.015625)
+    quant("x", 0, 128, a("xo"))
+    mm(0, "v", 0, "x", 0, 128)
+    store("A", T.oc[:], T.xq[:, 0:K].bitcast(dt.uint8), a("xq"))
+    for k in range(4):
+        store("SSSA"[k], T.osc[4 * k:4 * k + 4, :], T.xp[32 * k:32 * k + 4, 0:K], a("xp"))
+    copy(a("yt"), bank(0, 0, K))
+    store("A", T.y[:], T.yt[:], a("yt"))
+    for s in sorted(count):
+        need("G", (s, count[s]))

@@ -6,15 +6,15 @@ BF, F32, I32, U16, U8, X4 = "bfloat16", "float32", "int32", "uint16", "uint8", "
 SCRATCH = {"ps": ("psum", [128, 4096], F32)}
 for _d, _names in (
         (X4, "wq:512 uq:128 urq:128 zq:128 vq:128 qq:128 qrq:384 eq:512 hq:512 f0q:384 f1q:384 b1q:320 bq:128 xq:128 "
-             "l1q:192 l2q:192 l3q:176 r1q:64 r2q:64"),
+             "l1q:192 l2q:192 l3q:176 r1q:96 r2q:96"),
         (U8, "wp:512 up:128 urp:128 zp:128 vp:128 qp:128 qrp:384 ep:512 hp:512 f0p:384 f1p:384 b1p:320 bp:128 xp:128 "
-             "l1p:192 l2p:192 l3p:320 r1p:256 r2p:256"),
+             "l1p:192 l2p:192 l3p:176 r1p:192 r2p:192"),
         (BF, "xt:768 ut:512 zt:512 vt:512 qt:512 f0:768 t1:768 f1:768 t2:768 hs:1536 b1:512 bt:512 xo:512 gt:768 a0:192 "
-             "et:2048 zero:512 idn:128 ir:192 ip:192 jv:192 neg:192 one:16 m3:576 m4:192 c16:96 c16a:96 hm:48 "
-             "i0:580 i1:580 ex3:576 ex4:192 o0:192 o1:192 eb:384 eg:48 yg:96 nb:192 ya:194 yb:192 junk:576 "
+             "et:2048 zero:512 idn:128 ir:192 ip:192 jv:192 neg:192 one:128 m3:576 m4:192 c16:96 c16a:96 hm:48 "
+             "i0:580 i1:580 ex3:576 ex4:192 o0:192 o1:192 eb:384 eg:48 nb:192 ya:194 yb:192 junk:576 "
              "cm:582 rr:582 us:582 o4:768 c4:768"),
-        (F32, "xf:192 q64:192 yt:48 olt:48 olx:48 old:4 cf:8 cs:32 idf:128 eh:48 s0:12 s1:12 ye:96 "
-              "u0:12 u1:12 u2:12 u3:12 uc:4 sm:24"),
+        (F32, "xf:192 q64:192 yt:48 olt:48 olx:48 old:4 cf:8 cs:48 eh:48 s0:12 s1:12 yg:96 ye:96 c16x:96 "
+              "u0:12 u1:12 u2:12 u3:12 uc:4 sm:16"),
         (I32, "ci:48 cj:8"),
         (U16, "offu:8 offq:24 offe:4 p0:12 p1:12 g0:48 g1:48 so:6 m1:18 m2:12 j2:4 j4:12 "
               "lm1:18 lm2:12 lo1:48 lj:4 rm1:18 rm2:12 ro1:48")):
@@ -23,6 +23,7 @@ for _d, _names in (
 SEMAPHORES = ["nV", "nA", "nP", "nG", "dx", "du", "dq", "dz", "dv", "dwq", "dwp", "st", "ls",
               "a1", "a2", "a3", "am1", "am2", "ao", "aj", "h1", "h2", "hm1", "hm2", "ho"]
 ALU, ACT = AluOpType, ActivationFunctionType
+H = C // 2
 
 
 def _mask(engines):
@@ -34,7 +35,8 @@ def _mask(engines):
 
 def _helpers(topo, src, dst):
     h = [c for c in topo.cores_of(src) if c != src and topo.may_write(c, dst)]
-    return sorted(h, key=lambda c: (topo.die(c) != topo.die(src), c))
+    near, far = [c for c in h if topo.die(c) == topo.die(src)], [c for c in h if topo.die(c) != topo.die(src)]
+    return [near[0], far[0], near[1], far[1]]
 
 
 def _hand_on(g, core, T, topo):
@@ -44,9 +46,6 @@ def _hand_on(g, core, T, topo):
         return
     src, nxt, prv = T.cores[mine[0]], T.cores[(mine[0] + 1) % n], T.cores[(mine[0] - 1) % n]
     hs = _helpers(topo, src, nxt)
-    if core not in hs:
-        return
-    i = hs.index(core)
     full = len(topo.engines(src, core))
     sent = [0]
 
@@ -56,22 +55,18 @@ def _hand_on(g, core, T, topo):
         g.remote_dma(out, in_, T.sem[sem], T.sem.ls, pid, rid, topo.mask(core, dst))
         sent[0] += len(topo.engines(core, dst))
 
-    def tile(s):
-        if i < 3:
-            on("h" + s, full // len(hs), T["l%sq" % s][:, 64 * i:64 * i + 64].bitcast(dt.uint8),
+    for s in "12":
+        if core in hs[:2]:
+            i = hs.index(core)
+            on("h" + s, full // 2, T["l%sq" % s][:, H * i:H * i + H].bitcast(dt.uint8),
                T["r%sq" % s][:].bitcast(dt.uint8), "a" + s, nxt)
-        else:
-            on("h" + s, full // len(hs), T["l%sp" % s][:], T["r%sp" % s][:, 0:C], "a" + s, nxt)
-
-    tile("1")
-    if i == 0:
-        on("hm1", full, T.lm1[:], T.rm1[:], "am1", nxt)
-    tile("2")
-    if i == 0:
-        on("hm2", full, T.lm2[:], T.rm2[:], "am2", nxt)
-    if core == _helpers(topo, src, prv)[1]:
+        if core == hs[2]:
+            on("h" + s, full, T["l%sp" % s][:], T["r%sp" % s][:], "a" + s, nxt)
+            on("hm" + s, full, T["lm" + s][:], T["rm" + s][:], "am" + s, nxt)
+    if core == _helpers(topo, src, prv)[3]:
         on("ho", full, T.lo1[:], T.ro1[:], "ao", prv)
-    g.wait_ge(T.sem.ls, sent[0])
+    if sent[0]:
+        g.wait_ge(T.sem.ls, sent[0])
 
 
 def rank_program(g, core, T, topo):
@@ -177,11 +172,10 @@ def rank_program(g, core, T, topo):
     def copy(out, in_):
         op("V", lambda: g.vector.tensor_copy(out[0], in_[0]), [in_], [out])
 
-    def recip(out, in_):
-        op("V", lambda: g.vector.reciprocal(out[0], in_[0]), [in_], [out])
-
-    def gather(q, out, win, off, scale=None):
-        if q == "A":
+    def gather(q, out, win, off, scale=None, bias=None):
+        if bias is not None:
+            op("A", lambda: g.scalar.activation(out[0], win[0].indirect(off[0]), ACT.Identity, bias=bias), [win, off], [out])
+        elif q == "A":
             kw = {} if scale is None else {"scale": scale}
             op("A", lambda: g.scalar.activation(out[0], win[0].indirect(off[0]), ACT.Copy, **kw), [win, off], [out])
         elif scale is None:
@@ -194,6 +188,9 @@ def rank_program(g, core, T, topo):
             op("A", lambda: g.scalar.activation(out[0], in_[0], ACT.Copy, scale=s), [in_], [out])
         else:
             ts(out, in_, s, ALU.mult)
+
+    def zeros(name, lo, hi):
+        scaled("A", a(name, lo, hi), a("zero", 0, hi - lo), 1.0)
 
     def quant(nm, lo, w, tile):
         c, p = a(nm + "q", lo, lo + w), a(nm + "p", lo, lo + w)
@@ -217,34 +214,28 @@ def rank_program(g, core, T, topo):
         op("G", lambda: g.iota(out[0], pattern, base, cm, **kw), [], [out])
 
     hs = _helpers(topo, core, nxt)
-    back = _helpers(topo, core, prv)[1]
+    back = _helpers(topo, core, prv)[3]
+    near = topo.engines(core, hs[0])
 
     def send_tile(nm, s):
-        eng = topo.engines(core, hs[0])
-        half, moves = len(eng) // 2, []
-        for i, h in enumerate(hs):
-            e = eng[(i % 2) * half + i // 2:(i % 2) * half + half:2]
-            if i < 3:
-                r = a(nm + "q", 64 * i, 64 * i + 64)
-                moves.append((h, "h" + s, e, T["r%sq" % s][:].bitcast(dt.uint8), r[0].bitcast(dt.uint8), r))
-            else:
-                r = a(nm + "p", 0, 256)
-                moves.append((h, "h" + s, e, T["r%sp" % s][:], r[0], r))
-        send(moves)
+        r = [a(nm + "q", H * i, H * i + H) for i in range(2)]
+        send([(hs[i], "h" + s, near[i::2], T["r%sq" % s][:].bitcast(dt.uint8), r[i][0].bitcast(dt.uint8), r[i]) for i in range(2)])
+        p = a(nm + "p", 0, C)
+        send([(hs[2], "h" + s, near, T["r%sp" % s][:], p[0], p)])
 
     def via(src, i):
         return len(topo.engines(_helpers(topo, src, core)[i], core))
 
     direct = topo.engines(core, prv2)
-    lands("a1", sum(via(prv, i) for i in range(4)), a("l1q"), a("l1p"))
-    lands("a2", sum(via(prv, i) for i in range(4)), a("l2q"), a("l2p"))
-    lands("a3", len(topo.engines(nxt2, core)), a("l3q", 128, 176), a("l3p", 128, 320))
-    lands("am1", via(prv, 0), a("lm1"))
-    lands("am2", via(prv, 0), a("lm2"))
-    lands("ao", via(nxt, 1), a("lo1"))
+    lands("a1", sum(via(prv, i) for i in range(3)), a("l1q"), a("l1p"))
+    lands("a2", sum(via(prv, i) for i in range(3)), a("l2q"), a("l2p"))
+    lands("a3", 2 * len(topo.engines(nxt2, core)), a("l3q", 128, 176), a("l3p", 128, 176))
+    lands("am1", via(prv, 2), a("lm1"))
+    lands("am2", via(prv, 2), a("lm2"))
+    lands("ao", via(nxt, 3), a("lo1"))
     lands("aj", len(topo.engines(nxt2, core)), a("lj"))
 
-    load("A", "du", T.ut[:], T.u[:], a("ut"))
+    load("S", "du", T.ut[:], T.u[:], a("ut"))
     load("S", "dx", T.xt[:], T.x[:], a("xt"))
     need("S", ("dx", 16))
     load("S", "dq", T.qt[:, 0:C], T.q[:], a("qt", 0, C))
@@ -253,72 +244,82 @@ def rank_program(g, core, T, topo):
     load("S", "dwp", T.wp[:], T.ws[:], a("wp"))
     load("S", "dv", T.vt[:], T.v[:], a("vt"))
 
-    pm, sel, q4, sc3, sc4 = (a("cf", i, i + 1) for i in range(5))
+    pm, sel, q4, colb = (a("cf", i, i + 1) for i in range(4))
+    sc3, sc4 = a("cs", 31, 32), a("cs", 39, 40)
     iota(a("ci", 0, 1), [[0, 1]], 0, 1, False)
     iota(a("ci", 8, 16), [[16, 8]], 0, 0, False)
     iota(a("ir"), [[0, 12], [1, 16]], 0, 0, True)
-    iota(a("ip"), [[0, 48], [1, 4]], 0, 0, True)
-    iota(a("jv"), [[4, C]], 4, 0, True)
-    iota(a("idf"), [[1, 128]], 0, -1, True)
-    iota(a("ci", 16, 20), [[128, 4]], 0, 1, False)
-    iota(a("ci", 24, 48), [[16, 3], [0, 8]], 0, 0, False)
-    fill(a("et", 0, 512), 0.0)
-    fill(a("neg"), -1.0)
-    fill(a("i0", 0, 3), 256.0)
-    fill(a("one"), 1.0)
-    fill(a("o0"), 0.0)
-    for b in range(1, 4):
-        scaled("A", a("et", 512 * b, 512 * b + 512), a("et", 0, 512), 1.0)
+    fill(a("zero"), 0.0)
     ts(a("cj", 0, 1), a("ci", 0, 1), 15, ALU.bitwise_and)
-    ts(a("cj", 2, 3), a("ci", 0, 1), 3, ALU.bitwise_and)
+    fill(a("one"), 1.0)
     copy(a("offu"), a("ci", 8, 16))
     copy(pm, a("cj", 0, 1))
+    fill(a("neg"), -1.0)
     ts(a("cj", 1, 2), a("cj", 0, 1), 2, ALU.arith_shift_right)
-    ts(q4, a("cj", 2, 3), -4.0, ALU.add)
-    copy(sel, a("cj", 1, 2))
+    ts(a("cj", 2, 3), a("ci", 0, 1), 3, ALU.bitwise_and)
+    iota(a("ip"), [[0, 48], [1, 4]], 0, 0, True)
+    iota(a("jv"), [[4, C]], 4, 0, True)
+    op("G", lambda: g.affine_select(T.idn[:], T.one[:], [[-1, 128]], ALU.is_equal, 0.0, 0, 1), [a("one")], [a("idn")])
+    iota(a("ci", 24, 48), [[16, 3], [0, 8]], 0, 0, False)
+    iota(a("ci", 16, 20), [[128, 4]], 0, 1, False)
+    zeros("et", 0, 512)
+    zeros("o0", 0, C)
     ts(a("m3", 0, 576, 3), a("ir"), pm, ALU.is_gt, 4.0, ALU.mult)
-    ts(a("m3", 1, 576, 3), a("m3", 0, 576, 3), 257.0 / 1024, ALU.mult, -1.0 / 256, ALU.add)
-    scan(a("cs", 0, 16), a("m3", 0, 48, 3), a("neg", 0, 16), 0.0, ALU.mult, ALU.min)
-    ts(a("m3", 2, 576, 3), a("m3", 0, 576, 3), 64.25, ALU.mult, -256.0, ALU.add)
-    ts(a("m4"), a("ip"), sel, ALU.is_gt, 256.0, ALU.mult)
-    recip(sc3, a("cs", 15, 16))
-    scan(a("cs", 16, 20), a("m4", 0, 4), a("one", 0, 4), 0.0, ALU.mult, ALU.max)
-    recip(sc4, a("cs", 19, 20))
 
-    def counts(s, nnb, y, y2, last):
+    def counts(s, nnb, y, y2, last, spare):
         ts(nnb, s, 0.0, ALU.is_le, -1.0, ALU.mult)
+        gap(spare)
         scan(y, nnb, a("neg"), 256.0, ALU.add, ALU.max)
+        gap(spare)
         scan(y2, a("neg"), nnb, last, ALU.add, ALU.subtract)
+        gap(spare)
 
-    def sort(lv, s, t):
+    def gap(spare):
+        if spare:
+            spare.pop(0)()
+
+    def sort(lv, s, t, spare):
         i, p, o, gl, f = "i%d" % lv, a("p%d" % lv), a("o%d" % lv), "g%d" % lv, "f%d" % lv
-        counts(s, a(i, 4, 580, 3), a(i, 3, 579, 3), a(i, 5, 580, 3), a(i, 576, 577))
+        counts(s, a(i, 4, 580, 3), a(i, 3, 579, 3), a(i, 5, 580, 3), a(i, 576, 577), spare)
         scan(a("ex3"), a("m3"), a(i, 3, 579), 0.0, ALU.mult, ALU.max)
+        gap(spare)
         ts(p, a("ex3", 47, 576, 48), sc3, ALU.mult, 255.0, ALU.add)
+        gap(spare)
         op("V", lambda: g.vector.tensor_copy(o[0].indirect(p[0]), T.jv[:]), [p, a("jv")], [o])
+        gap(spare)
         scan(a("ex4"), a("m4"), o, 0.0, ALU.mult, ALU.max)
         ts(a(gl), a("ex4", 3, C, 4), sc4, ALU.mult, q4, ALU.add)
         gather("A", a(f, 384, 768), a(t), a(gl, 24, 48))
         gather("V", a(f, 0, 384), a(t), a(gl, 0, 24))
         quant(f, 0, C, a(f))
 
-    def step(lv, st, off, msg, wide):
+    def step(lv, st, off, msg, wide, spare):
         i = "i%d" % lv
-        gather("A", a("yg"), a(i, 0, 579), off)
+        gather("A", a("yg"), a(i, 0, 579), off, bias=1024.0)
         ts(a("uc", 3, 4), a(i, 576, 577), -1.0, ALU.mult, 256.0, ALU.add)
+        gap(spare)
         scan(a("ye"), a("yg"), a("c16"), 0.0, ALU.max, ALU.add)
-        ts(a("u0", 0, 6), a("ye", 15, 96, 16), -1.0, ALU.mult, -768.0, ALU.add)
+        gap(spare)
+        ts(a("u0", 0, 6), a("ye", 15, 96, 16), -1.0, ALU.mult, 256.0, ALU.add)
+        gap(spare)
         tt(a("u0", 6, 9), a("u0", 0, 3), a(st, 9, 12), ALU.add)
         tt(a("u1", 0, 6), a(st, 0, 6), a("u0", 0, 6), ALU.subtract)
         tt(a("u1", 6, 9), a(st, 6, 9), a("u0", 3, 6), ALU.subtract)
         tt(a("uc", 0, 3), a("u0", 6, 9), a("u0", 3, 6), ALU.is_ge)
+        gap(spare)
         for s in range(3):
             ts(a("u2", s, 9, 3), a("u1", s, 9, 3), a("uc", 3, 4), ALU.add, a("uc", s, s + 1), ALU.mult)
+        gap(spare)
         tt(a("u3", 0, 9), a("u0", 0, 9), a("u2", 0, 9), ALU.max)
+        gap(spare)
+        tt(a("u3", 9, 12), a("u3", 6, 9), a("u3", 0, 3), ALU.subtract)
         if wide:
             ts(a(msg, 0, 6), a("u3", 0, 6), 3.0, ALU.mult)
-        tt(a("u3", 9, 12), a("u3", 6, 9), a("u3", 0, 3), ALU.subtract)
+        gap(spare)
         copy(a(msg, 6, 18) if wide else a(msg), a("u3"))
+        send([(hs[2], "h" + msg, near, T["r" + msg][:], T[msg][:], a(msg))])
+        while spare:
+            gap(spare)
 
     def layer(land, t, nm, lo):
         for b in range(4):
@@ -327,73 +328,88 @@ def rank_program(g, core, T, topo):
             scaled("AV"[b % 2], a(t, b, 768, 4), bank(b, 0, C), 0.015625)
         quant(nm, lo, C, a(t))
 
+    def unit(nm):
+        return [lambda b=b: quant(nm, 128 * b, 128, a("et", 512 * b, 512 * b + 512)) for b in range(4)]
+
     quant("u", 0, 128, a("ut"))
+    ts(a("cs", 0, 16), a("m3", 0, 48, 3), -0.1875, ALU.mult, 1.0, ALU.add)
     pick("ur", "u", 128, a("offu"))
     quant("f0", C, C, a("xt"))
     mm(4, "ur", 0, "f0", C, C)
-    sort(0, bank(4, 0, C), "xt")
+    for b in range(1, 4):
+        zeros("et", 512 * b, 512 * b + 512)
+    zeros("qt", C, 512)
+    for b in range(2):
+        scaled("A", a("et", 512 * b + b, 512 * b + 512, 4), a("idn"), 64.0)
+    ts(a("m3", 1, 576, 3), a("m3", 0, 576, 3), 257.0 / 1024, ALU.mult, -1.0 / 256, ALU.add)
+    ts(a("m3", 2, 576, 3), a("m3", 0, 576, 3), 64.25, ALU.mult, -256.0, ALU.add)
+    copy(sel, a("cj", 1, 2))
+    sort(0, bank(4, 0, C), "xt", [
+        lambda: scan(a("cs", 16, 32), a("cs", 0, 16), a("one", 0, 16), -1.0, ALU.mult, ALU.mult),
+        lambda: ts(q4, a("cj", 2, 3), -4.0, ALU.add),
+        lambda: ts(a("m4"), a("ip"), sel, ALU.is_gt, 256.0, ALU.mult),
+        lambda: ts(a("cs", 32, 36), a("m4", 0, 4), -255.0 / 65536, ALU.mult, 1.0, ALU.add),
+        lambda: scan(a("cs", 36, 40), a("cs", 32, 36), a("one", 0, 4), 1.0, ALU.mult, ALU.mult),
+        lambda: ts(a("offq"), a("ci", 24, 48), pm, ALU.add)])
     send_tile("f0", "1")
 
-    ts(a("idn"), a("idf"), 0.0, ALU.is_equal)
-    for b in range(4):
-        scaled("A", a("et", 512 * b + b, 512 * b + 512, 4), a("idn"), 64.0)
-    fill(a("qt", C, 512), 0.0)
-    fill(a("i1", 0, 3), 256.0)
-    fill(a("o1"), 0.0)
-    ts(a("offq"), a("ci", 24, 48), pm, ALU.add)
-    copy(a("offe"), a("ci", 16, 20))
     quant("q", 0, 128, a("qt"))
     quant("z", 0, 128, a("zt"))
-    quant("e", 0, 512, a("et"))
     pick("qr", "q", 384, a("offq"))
+    for b in range(2, 4):
+        scaled("A", a("et", 512 * b + b, 512 * b + 512, 4), a("idn"), 64.0)
+    zeros("o1", 0, C)
     for c in range(3):
         mm(5 + c, "qr", 128 * c, "z", 0, 128)
     fill(a("hm"), 0.5)
-    ts(a("c16a"), a("ir", 0, 96), pm, ALU.is_lt, -1024.0, ALU.mult)
-    ts(a("c16"), a("ir", 0, 96), pm, ALU.is_equal, 1024.0, ALU.mult)
+    ts(a("c16a"), a("ir", 0, 96), pm, ALU.is_lt, -4096.0, ALU.mult)
+    ts(a("c16"), a("ir", 0, 96), pm, ALU.is_equal, 4096.0, ALU.mult)
+    copy(a("offe"), a("ci", 16, 20))
     fill(a("hm", 0, K, 16), 0.0)
     fill(a("hm", 6, K, 16), 0.0)
-    tt(a("c16"), a("c16"), a("c16a"), ALU.add)
     for c in range(3):
         ts(a("eb", 128 * c, 128 * c + 128), bank(5 + c, 0, 128), 0.0, ALU.is_gt)
-    ts(a("c16", 15, 96, 16), a("c16", 15, 96, 16), -2048.0, ALU.add)
+    tt(a("c16"), a("c16"), a("c16a"), ALU.add)
     gather("V", a("eg"), a("eb"), a("offe", 0, 3))
+    ts(a("c16", 15, 96, 16), a("c16", 15, 96, 16), -5120.0, ALU.add)
+    fill(a("i0", 0, 3), 256.0)
     scan(a("eh"), a("hm"), a("eg"), 0.0, ALU.mult, ALU.add)
+    fill(a("i1", 0, 3), 256.0)
     ts(a("s0", 0, 3), a("eh", 5, K, 16), 32.0, ALU.mult)
     ts(a("s0", 3, 6), a("eh", 5, K, 16), 32.0, ALU.mult, 128.0, ALU.add)
     ts(a("s0", 9, 12), a("eh", 12, K, 16), 64.0, ALU.mult)
     ts(a("so"), a("s0", 0, 6), 3.0, ALU.mult)
     tt(a("s0", 6, 9), a("s0", 0, 3), a("s0", 9, 12), ALU.add)
-    step(0, "s0", a("so"), "m1", True)
-    send([(hs[0], "hm1", topo.engines(core, hs[0]), T.rm1[:], T.m1[:], a("m1"))])
+    step(0, "s0", a("so"), "m1", True, unit("e"))
 
     layer("l1", "t1", "f1", C)
     mm(4, "ur", 0, "f1", C, C)
-    sort(1, bank(4, 0, C), "t1")
-    send_tile("f1", "2")
-    send([(back, "ho", topo.engines(core, back), T.ro1[:], T.g1[:], a("g1"))])
-    copy(a("s1"), a("lm1", 6, 18))
-    step(1, "s1", a("lm1", 0, 6), "m2", False)
-    send([(hs[0], "hm2", topo.engines(core, hs[0]), T.rm2[:], T.m2[:], a("m2"))])
-
     for b in range(4):
         scaled("A", a("et", 512 * b + b, 512 * b + 512, 4), a("idn"), 0.5)
+    for b in range(2):
+        zeros("hs", 512 * b, 512 * b + 512)
+    sort(1, bank(4, 0, C), "t1", [])
+    send_tile("f1", "2")
+    send([(back, "ho", near, T.ro1[:], T.g1[:], a("g1"))])
+    copy(a("s1"), a("lm1", 6, 18))
+    step(1, "s1", a("lm1", 0, 6), "m2", False, unit("h") + [
+        lambda: fill(a("cm", 192, 582, 194), 0.0), lambda: fill(a("cm", 193, 582, 194), -192.0),
+        lambda: fill(a("ya", 0, 1), 256.0)])
+
+    zeros("hs", 1024, 1536)
+    zeros("b1", C, 512)
+    zeros("o4", 0, 512)
+    zeros("o4", 512, 768)
+    zeros("bt", C, 512)
+    zeros("xo", C, 512)
     scaled("A", a("q64"), a("qt", 0, C), 64.0)
-    fill(a("hs"), 0.0)
-    fill(a("ya", 0, 1), 256.0)
     fill(a("rr"), 1.0)
-    fill(a("cm", 192, 582, 194), 0.0)
-    fill(a("cm", 193, 582, 194), -192.0)
-    fill(a("b1", C, 512), 0.0)
     fill(a("j2"), 0)
+    copy(a("c16x"), a("c16"))
+    ts(colb, a("c16", 15, 16), -255.5, ALU.add)
+    quant("l3", 0, 128, a("zero"))
     fill(a("rr", 0, 582, 194), 0.0)
     fill(a("rr", 192, 582, 194), 2.0)
-    quant("h", 0, 512, a("et"))
-    fill(a("zero"), 0.0)
-    fill(a("bt", C, 512), 0.0)
-    fill(a("xo", C, 512), 0.0)
-    fill(a("o4"), 0.0)
-    quant("l3", 0, 128, a("zero"))
     quant("v", 0, 128, a("vt"))
     ts(a("o4", 0, 768, 4), a("o0"), 0.25, ALU.mult, -1.0, ALU.add)
 
@@ -401,66 +417,67 @@ def rank_program(g, core, T, topo):
         scaled(q, a("hs", 384 * b, 384 * b + 384, 2), bank(4 + b, 0, C), 1.0)
 
     layer("l2", "t2", "b1", 128)
-    for b in range(4):
+    for b in range(3):
         mm(4 + b, "h", 128 * b, "l2", 0, C, True, False)
     mm(0, "ur", 0, "b1", 128, C)
     for b in range(4):
+        if b > 2:
+            mm(4 + b, "h", 128 * b, "l2", 0, C, True, False)
         mm(4 + b, "h", 128 * b, "b1", 128, C, False, True)
-    kf, kc, cb, bias, dd, sums = (a("sm", 4 * i, 4 * i + 3) for i in range(6))
-    copy(kf, a("lm2", 9, 12))
-    ts(kc, a("lm2", 9, 12), -1024.0, ALU.add)
+    cb, dd, mb = a("sm", 0, 3), a("sm", 4, 7), a("sm", 12, 15)
+    ts(a("c16x", 15, 48, 16), a("lm2", 9, 12), -1.0, ALU.mult, a("c16", 15, 16), ALU.add)
+    ts(mb, a("lm2", 6, 9), colb, ALU.add)
     hpart("A", 0)
-    counts(bank(0, 0, C), a("nb"), a("ya", 1, 193), a("yb"), a("ya", 192, 193))
-    gather("A", a("yg"), a("ya", 0, 193), a("lm2", 0, 6))
-    hpart("A", 1)
-    ts(cb, a("lm2", 6, 9), 768.5, ALU.add, a("ya", 192, 193), ALU.subtract)
+    counts(bank(0, 0, C), a("nb"), a("ya", 1, 193), a("yb"), a("ya", 192, 193), [])
+    gather("A", a("yg"), a("ya", 0, 193), a("lm2", 0, 6), bias=1024.0)
+    ts(a("c16x", 63, 96, 16), mb, a("ya", 192, 193), ALU.subtract)
     hpart("V", 2)
-    scan(a("ye"), a("yg"), a("c16"), 0.0, ALU.max, ALU.add)
-    el, eh = a("ye", 15, 48, 16), a("ye", 63, 96, 16)
-    tt(bias, eh, cb, ALU.add)
+    hpart("A", 1)
+    scan(a("ye"), a("yg"), a("c16x"), 0.0, ALU.max, ALU.add)
+    ts(cb, a("lm2", 6, 9), -255.5, ALU.add, a("ya", 192, 193), ALU.subtract)
     for s in range(3):
-        o, bc, ac = a("junk", C * s, C * s + C), a("sm", 12 + s, 13 + s), a("sm", 20 + s, 21 + s)
+        o, bc, ac = a("junk", C * s, C * s + C), a("ye", 63 + 16 * s, 64 + 16 * s), a("sm", 8 + s, 9 + s)
         op("A", lambda o=o, bc=bc, ac=ac: g.scalar.activation(o[0], T.yb[:], ACT.Sign, bias=bc[0], accum_out=ac[0]),
            [a("yb"), bc], [o, ac])
-    tt(dd, eh, kf, ALU.add)
     for s in range(3):
-        ts(a("cm", 194 * s, 194 * s + C), a("ya", 1, 193), a("sm", 4 + s, 5 + s), ALU.add,
-           a("ye", 16 * s + 15, 16 * s + 16), ALU.is_ge)
+        ts(a("cm", 194 * s, 194 * s + C), a("ya", 1, 193), a("ye", 16 * s + 15, 16 * s + 16), ALU.is_ge)
         if s == 0:
-            tt(a("rr", 193, 582, 194), dd, el, ALU.is_lt)
+            tt(dd, a("ye", 63, 96, 16), cb, ALU.subtract)
+        if s == 1:
+            tt(a("rr", 193, 582, 194), dd, a("ye", 15, 48, 16), ALU.is_lt)
     scan(a("us"), a("rr"), a("cm"), 0.0, ALU.mult, ALU.add)
-    hpart("V", 3)
+    hpart("A", 3)
     for s in range(3):
-        ts(a("j2", s, s + 1), a("sm", 20 + s, 21 + s), a("us", 194 * s + 193, 194 * s + 194), ALU.max, 192.0, ALU.add)
+        ts(a("j2", s, s + 1), a("sm", 8 + s, 9 + s), a("us", 194 * s + 193, 194 * s + 194), ALU.max, 192.0, ALU.add)
     send([(prv2, "aj", direct, T.lj[:], T.j2[:], a("j2"))])
     for b in range(4):
-        gather("AVAV"[b], a("b1", b, C, 4), a("hs", 384 * b, 384 * b + 384), a("j2", 0, 3))
+        gather("VVAA"[b], a("b1", b, C, 4), a("hs", 384 * b, 384 * b + 384), a("j2", 0, 3))
     quant("b1", 0, 128, a("b1"))
-    rc, rp = a("b1q", 0, K), a("b1p", 0, C)
-    send([(prv2, "a3", direct[0::2], T.l3q[:, 128:176].bitcast(dt.uint8), rc[0].bitcast(dt.uint8), rc),
-          (prv2, "a3", direct[1::2], T.l3p[:, 128:320], rp[0], rp)])
+    rc, rp = a("b1q", 0, K), a("b1p", 0, K)
+    send([(prv2, "a3", direct, T.l3q[:, 128:176].bitcast(dt.uint8), rc[0].bitcast(dt.uint8), rc)])
+    send([(prv2, "a3", direct, T.l3p[:, 128:176], rp[0], rp)])
 
     gather("A", a("gt", 384, 768), a("f0"), a("lo1", 24, 48))
     gather("V", a("gt", 0, 384), a("f0"), a("lo1", 0, 24))
     gather("A", a("c4", 384, 768), a("o4"), a("lo1", 24, 48))
-    gather("V", a("c4", 0, 384), a("o4"), a("lo1", 0, 24))
     for b in range(4):
         ts(a("j4", 3 * b, 3 * b + 3), a("lj", 0, 3), 2.0, ALU.mult, float(b), ALU.add)
-    gather("A", a("a0", 96, C), a("gt"), a("j4", 6, 12), 0.5)
-    gather("V", a("a0", 0, 96), a("gt"), a("j4", 0, 6), 0.5)
+    gather("V", a("a0"), a("gt"), a("j4"), 0.5)
+    gather("A", a("c4", 0, 384), a("o4"), a("lo1", 0, 24))
     gather("A", a("olt"), a("c4"), a("j4", 0, 3))
-    for c in range(3):
-        scan(a("olx", 16 * c, 16 * c + 16), a("olt", c, K, 3), a("c16", 0, 16), 0.0, ALU.max, ALU.add)
-    ts(a("old", 0, 3), a("olx", 15, K, 16), 1024.0, ALU.add)
-    store("S", T.ol[:], T.old[:, 0:3], a("old", 0, 3))
     for b in range(4):
         mm(b, "h", 128 * b, "l3", K, 128)
         tt(a("bt", b, C, 4), bank(b, 80, 128), a("a0", K * b, K * b + K), ALU.add)
     quant("b", 0, 128, a("bt"))
+    for c in range(3):
+        scan(a("olx", 16 * c, 16 * c + 16), a("olt", c, K, 3), a("c16", 0, 16), 0.0, ALU.max, ALU.add)
     for b in range(4):
         mm(4 + b, "w", 128 * b, "b", 0, 128)
         tt(a("xf", b, C, 4), bank(4 + b, 0, K), a("q64", b, C, 4), ALU.add)
         scaled("AAAV"[b], a("xo", b, C, 4), a("xf", b, C, 4), 0.015625)
+        if b == 0:
+            ts(a("old", 0, 3), a("olx", 15, K, 16), 1024.0, ALU.add)
+            store("S", T.ol[:], T.old[:, 0:3], a("old", 0, 3))
     quant("x", 0, 128, a("xo"))
     mm(0, "v", 0, "x", 0, 128)
     store("A", T.oc[:], T.xq[:, 0:K].bitcast(dt.uint8), a("xq"))

@@ -1,29 +1,28 @@
-from concourse.bass import DstId, RemoteDMATransfer
 from concourse.mybir import dt, AluOpType, ActivationFunctionType
 
 C, K = 192, 48
 BF, F32, I32, U16, U8, X4 = "bfloat16", "float32", "int32", "uint16", "uint8", "float8_e4m3fn_x4"
 SCRATCH = {"ps": ("psum", [128, 4096], F32)}
 for _d, _names in (
-        (X4, "wq:512 uq:128 urq:128 zq:128 vq:128 qq:128 qrq:384 eq:512 hq:512 f0q:384 f1q:384 b1q:320 bq:128 xq:128 "
+        (X4, "wq:512 uq:128 urq:128 zq:144 vq:128 qq:144 eq:512 hq:512 f0q:512 f1q:512 b1q:384 bq:128 xq:128 "
              "l1q:192 l2q:192 l3q:176 r1q:96 r2q:96"),
-        (U8, "wp:512 up:128 urp:128 zp:128 vp:128 qp:128 qrp:384 ep:512 hp:512 f0p:384 f1p:384 b1p:320 bp:128 xp:128 "
+        (U8, "wp:512 up:128 urp:128 zp:144 vp:128 qp:144 ep:512 hp:512 f0p:512 f1p:512 b1p:384 bp:128 xp:128 "
              "l1p:192 l2p:192 l3p:176 r1p:192 r2p:192"),
-        (BF, "xt:768 ut:512 zt:512 vt:512 qt:512 f0:768 t1:768 f1:768 t2:768 hs:1536 b1:512 bt:512 xo:512 gt:768 a0:192 "
-             "et:2048 zero:512 idn:128 ir:192 ip:192 jv:192 neg:192 one:128 m3:576 m4:192 c16:96 c16a:96 hm:48 "
-             "i0:580 i1:580 ex3:576 ex4:192 o0:192 o1:192 eb:384 eg:48 nb:192 ya:194 yb:192 junk:576 "
-             "cm:582 rr:582 us:582 o4:768 c4:768"),
-        (F32, "xf:192 q64:192 yt:48 olt:48 olx:48 old:4 cf:8 cs:48 eh:48 s0:12 s1:12 yg:96 ye:96 c16x:96 "
-              "u0:12 u1:12 u2:12 u3:12 uc:4 sm:16"),
-        (I32, "ci:48 cj:8"),
-        (U16, "offu:8 offq:24 offe:4 p0:12 p1:12 g0:48 g1:48 so:6 m1:18 m2:12 j2:4 j4:12 "
-              "lm1:18 lm2:12 lo1:48 lj:4 rm1:18 rm2:12 ro1:48")):
+        (BF, "xt:1024 ut:512 zt:576 vt:512 qt:192 qx:576 f0:1024 t1:1024 f1:1024 t2:1024 hs:768 b1:512 bt:512 xo:512 gt:768 "
+             "a0:192 et:515 ht:515 zero:576 ir:192 ip:192 jv:192 neg:192 one:16 m3:576 m4:192 c16:96 c16a:96 hm:96 "
+             "i0:580 i1:580 ex3:576 ex4:192 o0:192 o1:192 eb:96 eg:96 nb:192 ob:192 junk:576 "
+             "fz:576 fo:576 gz:576 hn:579 dj:579 us:579 far:4 o4:768 c4:768 m2:15 rm2:15 lm2:15"),
+        (F32, "xf:192 q64:192 yt:48 olt:48 olx:48 old:4 cf:8 cs:48 eh:96 s0:12 s1:12 yg:96 ye:96 "
+              "u0:12 u1:12 u2:12 u3:12 uc:4 sm:4"),
+        (I32, "ci:16 cj:8"),
+        (U16, "offu:8 p0:12 p1:12 g0:48 g1:48 so:6 m1:18 j2:4 j4:12 lm1:18 lo1:48 lj:4 rm1:18 ro1:48")):
     for _e in _names.split():
         SCRATCH[_e.split(":")[0]] = ("sbuf", [128, int(_e.split(":")[1])], _d)
-SEMAPHORES = ["nV", "nA", "nP", "nG", "dx", "du", "dq", "dz", "dv", "dwq", "dwp", "st", "ls",
+SEMAPHORES = ["nV", "nA", "nP", "nG", "dx", "du", "dq", "dz", "dz2", "dv", "dwq", "dwp", "st", "ls",
               "a1", "a2", "a3", "am1", "am2", "ao", "aj", "h1", "h2", "hm1", "hm2", "ho"]
 ALU, ACT = AluOpType, ActivationFunctionType
 H = C // 2
+PAD = 128 - H
 
 
 def _mask(engines):
@@ -36,7 +35,7 @@ def _mask(engines):
 def _helpers(topo, src, dst):
     h = [c for c in topo.cores_of(src) if c != src and topo.may_write(c, dst)]
     near, far = [c for c in h if topo.die(c) == topo.die(src)], [c for c in h if topo.die(c) != topo.die(src)]
-    return [near[0], far[0], near[1], far[1]]
+    return [far[0], near[0], near[1], far[1]]
 
 
 def _hand_on(g, core, T, topo):
@@ -58,7 +57,7 @@ def _hand_on(g, core, T, topo):
     for s in "12":
         if core in hs[:2]:
             i = hs.index(core)
-            on("h" + s, full // 2, T["l%sq" % s][:, H * i:H * i + H].bitcast(dt.uint8),
+            on("h" + s, full, T["l%sq" % s][:, H * i:H * i + H].bitcast(dt.uint8),
                T["r%sq" % s][:].bitcast(dt.uint8), "a" + s, nxt)
         if core == hs[2]:
             on("h" + s, full, T["l%sp" % s][:], T["r%sp" % s][:], "a" + s, nxt)
@@ -86,6 +85,10 @@ def rank_program(g, core, T, topo):
         if name == "ps":
             cols = range(lo // 512 * 512, lo // 512 * 512 + 512)
         return (T[name][:, lo:hi:step] if step != 1 else T[name][:, lo:hi], name, frozenset(cols))
+
+    def backwards(name, lo, hi, step=1):
+        last = lo + (hi - 1 - lo) // step * step
+        return (T[name][:, last:(lo - 1 if lo else None):-step], name, frozenset(range(lo, hi, step)))
 
     def need(q, tok):
         s, v = tok
@@ -135,20 +138,11 @@ def rank_program(g, core, T, topo):
         Q[q].dma_start(out, src).then_inc(T.sem.st, 16)
         count["st"] = count.get("st", 0) + 16
 
-    def send(moves):
-        order("G", [m[5] for m in moves], [])
-        if len(moves) == 1:
-            d, sem, eng, out, in_, _ = moves[0]
-            rid, pid = topo.addr(d, core)
-            g.remote_dma(out, in_, T.sem[sem], T.sem.ls, pid, rid, _mask(eng))
-        else:
-            tr = []
-            for d, sem, eng, out, in_, _ in moves:
-                rid, pid = topo.addr(d, core)
-                tr.append(RemoteDMATransfer(dst_ids=[DstId(rid=rid, pnc=pid)], dma_engine_mask=_mask(eng),
-                                            remote_sem=T.sem[sem], src=in_, dst=out))
-            g.remote_dma_fused(tr, local_sem=T.sem.ls)
-        count["ls"] = count.get("ls", 0) + sum(len(m[2]) for m in moves)
+    def send(d, sem, eng, out, in_, r):
+        order("G", [r], [])
+        rid, pid = topo.addr(d, core)
+        g.remote_dma(out, in_, T.sem[sem], T.sem.ls, pid, rid, _mask(eng))
+        count["ls"] = count.get("ls", 0) + len(eng)
 
     def sc(x):
         return (x[0], [x]) if isinstance(x, tuple) else (x, [])
@@ -192,6 +186,10 @@ def rank_program(g, core, T, topo):
     def zeros(name, lo, hi):
         scaled("A", a(name, lo, hi), a("zero", 0, hi - lo), 1.0)
 
+    def pads(name):
+        zeros(name, 0, 4 * PAD)
+        zeros(name, 4 * (PAD + C), 1024)
+
     def quant(nm, lo, w, tile):
         c, p = a(nm + "q", lo, lo + w), a(nm + "p", lo, lo + w)
         op("V", lambda: g.vector.quantize_mx(c[0], p[0], tile[0]), [tile], [c, p])
@@ -217,11 +215,13 @@ def rank_program(g, core, T, topo):
     back = _helpers(topo, core, prv)[3]
     near = topo.engines(core, hs[0])
 
-    def send_tile(nm, s):
-        r = [a(nm + "q", H * i, H * i + H) for i in range(2)]
-        send([(hs[i], "h" + s, near[i::2], T["r%sq" % s][:].bitcast(dt.uint8), r[i][0].bitcast(dt.uint8), r[i]) for i in range(2)])
-        p = a(nm + "p", 0, C)
-        send([(hs[2], "h" + s, near, T["r%sp" % s][:], p[0], p)])
+    def send_half(nm, s, i):
+        r = a(nm + "q", PAD + H * i, PAD + H * i + H)
+        send(hs[i], "h" + s, near, T["r%sq" % s][:].bitcast(dt.uint8), r[0].bitcast(dt.uint8), r)
+
+    def send_scales(nm, s):
+        p = a(nm + "p", PAD, PAD + C)
+        send(hs[2], "h" + s, near, T["r%sp" % s][:], p[0], p)
 
     def via(src, i):
         return len(topo.engines(_helpers(topo, src, core)[i], core))
@@ -236,51 +236,65 @@ def rank_program(g, core, T, topo):
     lands("aj", len(topo.engines(nxt2, core)), a("lj"))
 
     load("S", "du", T.ut[:], T.u[:], a("ut"))
-    load("S", "dx", T.xt[:], T.x[:], a("xt"))
+    load("S", "dx", T.xt[:, 0:4 * C], T.x[:], a("xt", 0, 4 * C))
     need("S", ("dx", 16))
-    load("S", "dq", T.qt[:, 0:C], T.q[:], a("qt", 0, C))
-    load("S", "dz", T.zt[:], T.z[:], a("zt"))
+    load("S", "dq", T.qt[:], T.q[:], a("qt"))
+    load("S", "dz", T.zt[:, 0:512], T.z[:], a("zt", 0, 512))
+    load("S", "dz2", T.zt[:, 512:576], T.z[:, 0:64], a("zt", 512, 576))
     load("S", "dwq", T.wq[:].bitcast(dt.uint8), T.wc[:], a("wq"))
     load("S", "dwp", T.wp[:], T.ws[:], a("wp"))
     load("S", "dv", T.vt[:], T.v[:], a("vt"))
 
-    pm, sel, q4, colb = (a("cf", i, i + 1) for i in range(4))
+    pm, sel, q4 = (a("cf", i, i + 1) for i in range(3))
     sc3, sc4 = a("cs", 31, 32), a("cs", 39, 40)
     iota(a("ci", 0, 1), [[0, 1]], 0, 1, False)
     iota(a("ci", 8, 16), [[16, 8]], 0, 0, False)
     iota(a("ir"), [[0, 12], [1, 16]], 0, 0, True)
     fill(a("zero"), 0.0)
     ts(a("cj", 0, 1), a("ci", 0, 1), 15, ALU.bitwise_and)
-    fill(a("one"), 1.0)
-    copy(a("offu"), a("ci", 8, 16))
-    copy(pm, a("cj", 0, 1))
-    fill(a("neg"), -1.0)
-    ts(a("cj", 1, 2), a("cj", 0, 1), 2, ALU.arith_shift_right)
+    ts(a("cj", 1, 2), a("ci", 0, 1), 15, ALU.bitwise_and, 2, ALU.arith_shift_right)
     ts(a("cj", 2, 3), a("ci", 0, 1), 3, ALU.bitwise_and)
+    fill(a("hm"), 0.5)
+    copy(a("offu"), a("ci", 8, 16))
+    copy(a("cf", 0, 2), a("cj", 0, 2))
+    fill(a("neg"), -1.0)
+    fill(a("one"), 1.0)
+    ts(q4, a("cj", 2, 3), -4.0, ALU.add)
+    fill(a("hm", 0, 96, 32), 0.0)
+    fill(a("hm", 6, 96, 32), 0.0)
     iota(a("ip"), [[0, 48], [1, 4]], 0, 0, True)
     iota(a("jv"), [[4, C]], 4, 0, True)
-    op("G", lambda: g.affine_select(T.idn[:], T.one[:], [[-1, 128]], ALU.is_equal, 0.0, 0, 1), [a("one")], [a("idn")])
-    iota(a("ci", 24, 48), [[16, 3], [0, 8]], 0, 0, False)
-    iota(a("ci", 16, 20), [[128, 4]], 0, 1, False)
-    zeros("et", 0, 512)
-    zeros("o0", 0, C)
-    ts(a("m3", 0, 576, 3), a("ir"), pm, ALU.is_gt, 4.0, ALU.mult)
 
-    def counts(s, nnb, y, y2, last, spare):
-        ts(nnb, s, 0.0, ALU.is_le, -1.0, ALU.mult)
-        gap(spare)
-        scan(y, nnb, a("neg"), 256.0, ALU.add, ALU.max)
-        gap(spare)
-        scan(y2, a("neg"), nnb, last, ALU.add, ALU.subtract)
-        gap(spare)
+    def diagonal(name, v):
+        op("G", lambda: g.affine_select(T[name][:], T.zero[:, 0:515], [[-1, 515]], ALU.not_equal, v, 3, 4), [a("zero")], [a(name)])
+
+    diagonal("et", 64.0)
+    zeros("xt", 4 * C, 1024)
+    zeros("o0", 0, C)
+    pads("f0")
+
+    def scores(b, nm, lo, t):
+        for h in range(2):
+            quant(nm, lo + 128 * h, 128, a(t, 512 * h, 512 * h + 512))
+            mm(b + h, "ur", 0, nm, lo + 128 * h, 128)
+
+    def bits(b, h, nm, lo, step, cmp, factor):
+        w = (128, C - 128)[h]
+        ts(a(nm, lo + 128 * h * step, lo + (128 * h + w) * step, step), bank(b + h, 0, w), 0.0, cmp, factor, ALU.mult)
 
     def gap(spare):
         if spare:
-            spare.pop(0)()
+            for call in spare.pop(0):
+                call()
 
-    def sort(lv, s, t, spare):
-        i, p, o, gl, f = "i%d" % lv, a("p%d" % lv), a("o%d" % lv), "g%d" % lv, "f%d" % lv
-        counts(s, a(i, 4, 580, 3), a(i, 3, 579, 3), a(i, 5, 580, 3), a(i, 576, 577), spare)
+    def sort(lv, b, t, spare):
+        i, p, o, gl, f, to = "i%d" % lv, a("p%d" % lv), a("o%d" % lv), "g%d" % lv, "f%d" % lv, str(lv + 1)
+        for h in range(2):
+            bits(b, h, i, 4, 3, ALU.is_le, -1.0)
+        gap(spare)
+        scan(a(i, 3, 579, 3), a(i, 4, 580, 3), a("neg"), 256.0, ALU.add, ALU.max)
+        scan(backwards(i, 5, 580, 3), backwards(i, 4, 580, 3), a("neg"), 255.0 - C, ALU.add, ALU.subtract)
+        gap(spare)
         scan(a("ex3"), a("m3"), a(i, 3, 579), 0.0, ALU.mult, ALU.max)
         gap(spare)
         ts(p, a("ex3", 47, 576, 48), sc3, ALU.mult, 255.0, ALU.add)
@@ -288,182 +302,198 @@ def rank_program(g, core, T, topo):
         op("V", lambda: g.vector.tensor_copy(o[0].indirect(p[0]), T.jv[:]), [p, a("jv")], [o])
         gap(spare)
         scan(a("ex4"), a("m4"), o, 0.0, ALU.mult, ALU.max)
+        gap(spare)
         ts(a(gl), a("ex4", 3, C, 4), sc4, ALU.mult, q4, ALU.add)
-        gather("A", a(f, 384, 768), a(t), a(gl, 24, 48))
-        gather("V", a(f, 0, 384), a(t), a(gl, 0, 24))
-        quant(f, 0, C, a(f))
+        if lv:
+            send(back, "ho", near, T.ro1[:], T.g1[:], a("g1"))
+        gap(spare)
 
-    def step(lv, st, off, msg, wide, spare):
-        i = "i%d" % lv
-        gather("A", a("yg"), a(i, 0, 579), off, bias=1024.0)
-        ts(a("uc", 3, 4), a(i, 576, 577), -1.0, ALU.mult, 256.0, ALU.add)
-        gap(spare)
-        scan(a("ye"), a("yg"), a("c16"), 0.0, ALU.max, ALU.add)
-        gap(spare)
-        ts(a("u0", 0, 6), a("ye", 15, 96, 16), -1.0, ALU.mult, 256.0, ALU.add)
-        gap(spare)
-        tt(a("u0", 6, 9), a("u0", 0, 3), a(st, 9, 12), ALU.add)
-        tt(a("u1", 0, 6), a(st, 0, 6), a("u0", 0, 6), ALU.subtract)
-        tt(a("u1", 6, 9), a(st, 6, 9), a("u0", 3, 6), ALU.subtract)
-        tt(a("uc", 0, 3), a("u0", 6, 9), a("u0", 3, 6), ALU.is_ge)
-        gap(spare)
-        for s in range(3):
-            ts(a("u2", s, 9, 3), a("u1", s, 9, 3), a("uc", 3, 4), ALU.add, a("uc", s, s + 1), ALU.mult)
-        gap(spare)
-        tt(a("u3", 0, 9), a("u0", 0, 9), a("u2", 0, 9), ALU.max)
-        gap(spare)
-        tt(a("u3", 9, 12), a("u3", 6, 9), a("u3", 0, 3), ALU.subtract)
-        if wide:
-            ts(a(msg, 0, 6), a("u3", 0, 6), 3.0, ALU.mult)
-        gap(spare)
-        copy(a(msg, 6, 18) if wide else a(msg), a("u3"))
-        send([(hs[2], "h" + msg, near, T["r" + msg][:], T[msg][:], a(msg))])
-        while spare:
-            gap(spare)
+        def part(q, lo, hi):
+            gather(q, a(f, 4 * PAD + 16 * lo, 4 * PAD + 16 * hi), a(t, 0, 4 * C), a(gl, lo, hi))
 
-    def layer(land, t, nm, lo):
+        part("A", 12, 24)
+        part("V", 0, 12)
+        part("A", 32, 48)
+        gap(spare)
+        quant(f, 0, 128, a(f, 0, 512))
+        send_half(f, to, 0)
+        part("V", 24, 32)
+        gap(spare)
+        quant(f, 128, 128, a(f, 512, 1024))
+        send_half(f, to, 1)
+        send_scales(f, to)
+
+    def step(lv, st, off, msg):
+        i, ye = "i%d" % lv, a("ye", 15, 96, 16)
+        if lv:
+            last = [[lambda: ts(a(msg, 0, 6), a("u3", 0, 6), 4.0, ALU.mult, 4.0, ALU.add),
+                     lambda: tt(a(msg, 9, 12), a("u3", 6, 9), a("u3", 3, 6), ALU.subtract),
+                     lambda: ts(a(msg, 12, 15), a("u3", 3, 6), -256.0, ALU.mult, 256.0, ALU.add)] +
+                    [lambda s=s: ts(a(msg, 6 + s, 7 + s), a("u3", 6 + s, 7 + s), a("u3", s, s + 1), ALU.subtract, 1.0, ALU.add)
+                     for s in range(3)]]
+        else:
+            last = [[lambda: tt(a("u3", 9, 12), a("u3", 6, 9), a("u3", 0, 3), ALU.subtract),
+                     lambda: ts(a(msg, 0, 6), a("u3", 0, 6), 3.0, ALU.mult)],
+                    [lambda: copy(a(msg, 6, 18), a("u3", 0, 12))]]
+        last[-1].append(lambda: send(hs[2], "h" + msg, near, T["r" + msg][:], T[msg][:], a(msg)))
+        return [
+            [lambda: gather("A", a("yg"), a(i, 0, 579), off, bias=1024.0),
+             lambda: ts(a("uc", 3, 4), a(i, 576, 577), -1.0, ALU.mult, 256.0, ALU.add)],
+            [lambda: scan(a("ye"), a("yg"), a("c16"), 0.0, ALU.max, ALU.add)],
+            [lambda: tt(a("u0", 9, 12), a("ye", 15, 48, 16), a(st, 9, 12), ALU.subtract),
+             lambda: tt(a("u1", 0, 6), a(st, 0, 6), ye, ALU.add),
+             lambda: tt(a("u1", 6, 9), a(st, 6, 9), a("ye", 63, 96, 16), ALU.add)],
+            [lambda: ts(a("u0", 0, 6), ye, -1.0, ALU.mult, 256.0, ALU.add),
+             lambda: tt(a("uc", 0, 3), a("u0", 9, 12), a("ye", 63, 96, 16), ALU.is_le),
+             lambda: ts(a("u0", 6, 9), a("u0", 9, 12), -1.0, ALU.mult, 256.0, ALU.add)],
+            [lambda s=s: ts(a("u2", s, 9, 3), a("u1", s, 9, 3), a("uc", 3, 4), ALU.add, a("uc", s, s + 1), ALU.mult)
+             for s in range(3)],
+            [lambda: tt(a("u3", 0, 9), a("u0", 0, 9), a("u2", 0, 9), ALU.max)]] + last
+
+    def layer(land, t, spare):
         for b in range(4):
             mm(b, "w", 128 * b, land, 0, C, True, False)
             mm(b, "e", 128 * b, land, 0, C, False, True)
-            scaled("AV"[b % 2], a(t, b, 768, 4), bank(b, 0, C), 0.015625)
-        quant(nm, lo, C, a(t))
+            if b < 3:
+                scaled("A", a(t, b, 4 * C, 4), bank(b, 0, C), 0.015625)
+        gap([spare])
+        scaled("V", a(t, 3, 512, 4), bank(3, 0, 128), 0.015625)
+        scaled("V", a(t, 515, 4 * C, 4), bank(3, 128, C), 0.015625)
 
     def unit(nm):
-        return [lambda b=b: quant(nm, 128 * b, 128, a("et", 512 * b, 512 * b + 512)) for b in range(4)]
+        return [[lambda b=b: quant(nm, 128 * b, 128, a(nm + "t", 3 - b, 515 - b))] for b in range(4)]
+
+    def query_scores():
+        quant("q", 0, 144, a("qx"))
+        mm(6, "z", 0, "q", 16, 128, True, False)
+        mm(6, "z", 16, "q", 0, 128, False, True)
 
     quant("u", 0, 128, a("ut"))
-    ts(a("cs", 0, 16), a("m3", 0, 48, 3), -0.1875, ALU.mult, 1.0, ALU.add)
+    ts(a("m3", 0, 576, 3), a("ir"), pm, ALU.is_gt, 4.0, ALU.mult)
     pick("ur", "u", 128, a("offu"))
-    quant("f0", C, C, a("xt"))
-    mm(4, "ur", 0, "f0", C, C)
-    for b in range(1, 4):
-        zeros("et", 512 * b, 512 * b + 512)
-    zeros("qt", C, 512)
-    for b in range(2):
-        scaled("A", a("et", 512 * b + b, 512 * b + 512, 4), a("idn"), 64.0)
+    ts(a("cs", 0, 16), a("m3", 0, 48, 3), -0.1875, ALU.mult, 1.0, ALU.add)
+    scores(4, "f0", 256, "xt")
+    zeros("qx", 0, 576)
+    zeros("o1", 0, C)
+    pads("f1")
+    for t in ("t1", "t2"):
+        zeros(t, 4 * C, 1024)
+    zeros("b1", C, 512)
+    for c in range(3):
+        scaled("A", a("qx", 64 + 128 * c, 128 + 128 * c), a("qt", 64 * c, 64 * c + 64), 1.0)
     ts(a("m3", 1, 576, 3), a("m3", 0, 576, 3), 257.0 / 1024, ALU.mult, -1.0 / 256, ALU.add)
     ts(a("m3", 2, 576, 3), a("m3", 0, 576, 3), 64.25, ALU.mult, -256.0, ALU.add)
-    copy(sel, a("cj", 1, 2))
-    sort(0, bank(4, 0, C), "xt", [
-        lambda: scan(a("cs", 16, 32), a("cs", 0, 16), a("one", 0, 16), -1.0, ALU.mult, ALU.mult),
-        lambda: ts(q4, a("cj", 2, 3), -4.0, ALU.add),
-        lambda: ts(a("m4"), a("ip"), sel, ALU.is_gt, 256.0, ALU.mult),
-        lambda: ts(a("cs", 32, 36), a("m4", 0, 4), -255.0 / 65536, ALU.mult, 1.0, ALU.add),
-        lambda: scan(a("cs", 36, 40), a("cs", 32, 36), a("one", 0, 4), 1.0, ALU.mult, ALU.mult),
-        lambda: ts(a("offq"), a("ci", 24, 48), pm, ALU.add)])
-    send_tile("f0", "1")
+    ts(a("m4"), a("ip"), sel, ALU.is_gt, 256.0, ALU.mult)
+    sort(0, 4, "xt", [
+        [lambda: scan(a("cs", 16, 32), a("cs", 0, 16), a("one", 0, 16), -1.0, ALU.mult, ALU.mult)],
+        [lambda: ts(a("cs", 32, 36), a("m4", 0, 4), -255.0 / 65536, ALU.mult, 1.0, ALU.add)],
+        [lambda: scan(a("cs", 36, 40), a("cs", 32, 36), a("one", 0, 4), 1.0, ALU.mult, ALU.mult)],
+        [lambda: ts(a("c16a"), a("ir", 0, 96), pm, ALU.is_lt, -4096.0, ALU.mult)],
+        [lambda: quant("z", 0, 144, a("zt"))],
+        [query_scores],
+        [lambda: ts(a("c16"), a("ir", 0, 96), pm, ALU.is_equal, 4096.0, ALU.mult)],
+        [lambda: ts(a("eb"), bank(6, 0, 96), 0.0, ALU.is_gt)],
+        [lambda: op("V", lambda: g.vector.transpose(T.eg[:], T.eb[:]), [a("eb")], [a("eg")])]])
 
-    quant("q", 0, 128, a("qt"))
-    quant("z", 0, 128, a("zt"))
-    pick("qr", "q", 384, a("offq"))
-    for b in range(2, 4):
-        scaled("A", a("et", 512 * b + b, 512 * b + 512, 4), a("idn"), 64.0)
-    zeros("o1", 0, C)
-    for c in range(3):
-        mm(5 + c, "qr", 128 * c, "z", 0, 128)
-    fill(a("hm"), 0.5)
-    ts(a("c16a"), a("ir", 0, 96), pm, ALU.is_lt, -4096.0, ALU.mult)
-    ts(a("c16"), a("ir", 0, 96), pm, ALU.is_equal, 4096.0, ALU.mult)
-    copy(a("offe"), a("ci", 16, 20))
-    fill(a("hm", 0, K, 16), 0.0)
-    fill(a("hm", 6, K, 16), 0.0)
-    for c in range(3):
-        ts(a("eb", 128 * c, 128 * c + 128), bank(5 + c, 0, 128), 0.0, ALU.is_gt)
-    tt(a("c16"), a("c16"), a("c16a"), ALU.add)
-    gather("V", a("eg"), a("eb"), a("offe", 0, 3))
-    ts(a("c16", 15, 96, 16), a("c16", 15, 96, 16), -5120.0, ALU.add)
-    fill(a("i0", 0, 3), 256.0)
+    first, e = step(0, "s0", a("so"), "m1"), unit("e")
+    lo, k = a("eh", 5, 96, 32), a("eh", 12, 96, 32)
     scan(a("eh"), a("hm"), a("eg"), 0.0, ALU.mult, ALU.add)
-    fill(a("i1", 0, 3), 256.0)
-    ts(a("s0", 0, 3), a("eh", 5, K, 16), 32.0, ALU.mult)
-    ts(a("s0", 3, 6), a("eh", 5, K, 16), 32.0, ALU.mult, 128.0, ALU.add)
-    ts(a("s0", 9, 12), a("eh", 12, K, 16), 64.0, ALU.mult)
-    ts(a("so"), a("s0", 0, 6), 3.0, ALU.mult)
+    tt(a("c16"), a("c16"), a("c16a"), ALU.add)
+    ts(a("so", 0, 3), lo, 96.0, ALU.mult)
+    ts(a("so", 3, 6), lo, 96.0, ALU.mult, 384.0, ALU.add)
+    fill(a("i0", 0, 3), 256.0)
+    gap(first)
+    ts(a("c16", 15, 96, 16), a("c16", 15, 96, 16), -5120.0, ALU.add)
+    ts(a("s0", 0, 3), lo, 32.0, ALU.mult, -256.0, ALU.add)
+    ts(a("s0", 9, 12), k, 64.0, ALU.mult)
+    ts(a("s0", 3, 6), lo, 32.0, ALU.mult, -128.0, ALU.add)
+    gap(e)
     tt(a("s0", 6, 9), a("s0", 0, 3), a("s0", 9, 12), ALU.add)
-    step(0, "s0", a("so"), "m1", True, unit("e"))
-
-    layer("l1", "t1", "f1", C)
-    mm(4, "ur", 0, "f1", C, C)
-    for b in range(4):
-        scaled("A", a("et", 512 * b + b, 512 * b + 512, 4), a("idn"), 0.5)
-    for b in range(2):
-        zeros("hs", 512 * b, 512 * b + 512)
-    sort(1, bank(4, 0, C), "t1", [])
-    send_tile("f1", "2")
-    send([(back, "ho", near, T.ro1[:], T.g1[:], a("g1"))])
-    copy(a("s1"), a("lm1", 6, 18))
-    step(1, "s1", a("lm1", 0, 6), "m2", False, unit("h") + [
-        lambda: fill(a("cm", 192, 582, 194), 0.0), lambda: fill(a("cm", 193, 582, 194), -192.0),
-        lambda: fill(a("ya", 0, 1), 256.0)])
-
-    zeros("hs", 1024, 1536)
-    zeros("b1", C, 512)
-    zeros("o4", 0, 512)
-    zeros("o4", 512, 768)
-    zeros("bt", C, 512)
-    zeros("xo", C, 512)
+    zeros("o4", 0, 384)
+    zeros("o4", 384, 768)
+    for t in ("bt", "xo"):
+        zeros(t, C, 512)
     scaled("A", a("q64"), a("qt", 0, C), 64.0)
-    fill(a("rr"), 1.0)
-    fill(a("j2"), 0)
-    copy(a("c16x"), a("c16"))
-    ts(colb, a("c16", 15, 16), -255.5, ALU.add)
-    quant("l3", 0, 128, a("zero"))
-    fill(a("rr", 0, 582, 194), 0.0)
-    fill(a("rr", 192, 582, 194), 2.0)
-    quant("v", 0, 128, a("vt"))
+    e += [[lambda: quant("l3", 0, 128, a("zero", 0, 512))], [lambda: quant("v", 0, 128, a("vt"))],
+          [lambda: fill(a("hn", 0, 579, C + 1), -512.0), lambda: fill(a("j2"), 0), lambda: fill(a("i1", 0, 3), 256.0)]]
+    while first or e:
+        gap(first)
+        gap(e)
+    diagonal("ht", 0.5)
+    iota(a("dj"), [[0, 3], [-1, C + 1]], C - 1, 0, True)
+
+    layer("l1", "t1", [])
+    scores(4, "f1", 256, "t1")
+    second = step(1, "s1", a("lm1", 0, 6), "m2")
+    pick_y, all_zeros = second.pop(0)
+    calls = [call for group in second[1:4] for call in group]
+    sort(1, 4, "t1", [
+        [lambda: ts(a("s1", 0, 9), a("lm1", 6, 15), -256.0, ALU.add)],
+        [pick_y, lambda: copy(a("s1", 9, 12), a("lm1", 15, 18))],
+        [all_zeros], second[0]] + [calls[i:i + 2] for i in range(0, 9, 2)])
+
+    for group in second[4:] + unit("h"):
+        gap([group])
+    for h in range(2):
+        gather("A", a("gt", 384 * h, 384 * h + 384), a("f0", 4 * PAD, 4 * (PAD + C)), a("lo1", 24 * h, 24 * h + 24))
     ts(a("o4", 0, 768, 4), a("o0"), 0.25, ALU.mult, -1.0, ALU.add)
 
     def hpart(q, b):
-        scaled(q, a("hs", 384 * b, 384 * b + 384, 2), bank(4 + b, 0, C), 1.0)
+        scaled(q, a("hs", C * b, C * b + C), bank(4 + b, 0, C), 1.0)
 
-    layer("l2", "t2", "b1", 128)
-    for b in range(3):
+    def col(i, s):
+        return a("lm2", 3 * i + s, 3 * i + s + 1)
+
+    def hold_ones(s):
+        ts(a("fo", C * s, C * s + C), a("jv"), col(1, s), ALU.is_ge, col(3, s), ALU.mult)
+
+    layer("l2", "t2", [
+        lambda s=s: ts(a("fz", C * s, C * s + C), a("jv"), col(0, s), ALU.is_lt, col(2, s), ALU.mult) for s in range(3)])
+    for b in range(2):
         mm(4 + b, "h", 128 * b, "l2", 0, C, True, False)
-    mm(0, "ur", 0, "b1", 128, C)
+    scores(0, "b1", 128, "t2")
+    hold_ones(0)
+    hold_ones(1)
     for b in range(4):
-        if b > 2:
+        if b >= 2:
             mm(4 + b, "h", 128 * b, "l2", 0, C, True, False)
         mm(4 + b, "h", 128 * b, "b1", 128, C, False, True)
-    cb, dd, mb = a("sm", 0, 3), a("sm", 4, 7), a("sm", 12, 15)
-    ts(a("c16x", 15, 48, 16), a("lm2", 9, 12), -1.0, ALU.mult, a("c16", 15, 16), ALU.add)
-    ts(mb, a("lm2", 6, 9), colb, ALU.add)
+    for h in range(2):
+        bits(0, h, "nb", 0, 1, ALU.is_le, -1.0)
+        bits(0, h, "ob", 0, 1, ALU.is_gt, 1.0)
+    hold_ones(2)
     hpart("A", 0)
-    counts(bank(0, 0, C), a("nb"), a("ya", 1, 193), a("yb"), a("ya", 192, 193), [])
-    gather("A", a("yg"), a("ya", 0, 193), a("lm2", 0, 6), bias=1024.0)
-    ts(a("c16x", 63, 96, 16), mb, a("ya", 192, 193), ALU.subtract)
-    hpart("V", 2)
-    hpart("A", 1)
-    scan(a("ye"), a("yg"), a("c16x"), 0.0, ALU.max, ALU.add)
-    ts(cb, a("lm2", 6, 9), -255.5, ALU.add, a("ya", 192, 193), ALU.subtract)
     for s in range(3):
-        o, bc, ac = a("junk", C * s, C * s + C), a("ye", 63 + 16 * s, 64 + 16 * s), a("sm", 8 + s, 9 + s)
-        op("A", lambda o=o, bc=bc, ac=ac: g.scalar.activation(o[0], T.yb[:], ACT.Sign, bias=bc[0], accum_out=ac[0]),
-           [a("yb"), bc], [o, ac])
+        scan(a("gz", C * s, C * s + C), a("nb"), a("fz", C * s, C * s + C), col(2, s), ALU.add, ALU.max)
     for s in range(3):
-        ts(a("cm", 194 * s, 194 * s + C), a("ya", 1, 193), a("ye", 16 * s + 15, 16 * s + 16), ALU.is_ge)
-        if s == 0:
-            tt(dd, a("ye", 63, 96, 16), cb, ALU.subtract)
-        if s == 1:
-            tt(a("rr", 193, 582, 194), dd, a("ye", 15, 48, 16), ALU.is_lt)
-    scan(a("us"), a("rr"), a("cm"), 0.0, ALU.mult, ALU.add)
+        scan(a("hn", (C + 1) * s + 1, (C + 1) * (s + 1)), backwards("ob", 0, C), backwards("fo", C * s, C * s + C), col(3, s),
+             ALU.add, ALU.min)
+    for s in range(3):
+        o, x, ac = a("junk", C * s, C * s + C), a("gz", C * s, C * s + C), a("sm", s, s + 1)
+        op("A", lambda o=o, x=x, ac=ac: g.scalar.activation(o[0], x[0], ACT.Sign, accum_out=ac[0]), [x], [o, ac])
+    for s in range(3):
+        o, x, bc = a("far", s, s + 1), a("sm", s, s + 1), col(4, s)
+        op("A", lambda o=o, x=x, bc=bc: g.scalar.activation(o[0], x[0], ACT.Relu, bias=bc[0], scale=256.0), [x, bc], [o])
+    scaled("V", a("hs", C, C + H), bank(5, 0, H), 1.0)
+    scan(a("us"), a("hn"), a("dj"), 0.0, ALU.add, ALU.max)
+    scaled("V", a("hs", C + H, 2 * C), bank(5, H, C), 1.0)
+    hpart("A", 2)
     hpart("A", 3)
     for s in range(3):
-        ts(a("j2", s, s + 1), a("sm", 8 + s, 9 + s), a("us", 194 * s + 193, 194 * s + 194), ALU.max, 192.0, ALU.add)
-    send([(prv2, "aj", direct, T.lj[:], T.j2[:], a("j2"))])
+        ts(a("j2", s, s + 1), a("sm", s, s + 1), a("far", s, s + 1), ALU.subtract, a("us", (C + 1) * s + C, (C + 1) * (s + 1)), ALU.max)
+    send(prv2, "aj", direct, T.lj[:], T.j2[:], a("j2"))
     for b in range(4):
-        gather("VVAA"[b], a("b1", b, C, 4), a("hs", 384 * b, 384 * b + 384), a("j2", 0, 3))
+        gather("VVAA"[b], a("b1", b, C, 4), a("hs", C * b, C * b + C), a("j2", 0, 3))
     quant("b1", 0, 128, a("b1"))
     rc, rp = a("b1q", 0, K), a("b1p", 0, K)
-    send([(prv2, "a3", direct, T.l3q[:, 128:176].bitcast(dt.uint8), rc[0].bitcast(dt.uint8), rc)])
-    send([(prv2, "a3", direct, T.l3p[:, 128:176], rp[0], rp)])
+    send(prv2, "a3", direct, T.l3q[:, 128:176].bitcast(dt.uint8), rc[0].bitcast(dt.uint8), rc)
+    send(prv2, "a3", direct, T.l3p[:, 128:176], rp[0], rp)
 
-    gather("A", a("gt", 384, 768), a("f0"), a("lo1", 24, 48))
-    gather("V", a("gt", 0, 384), a("f0"), a("lo1", 0, 24))
     gather("A", a("c4", 384, 768), a("o4"), a("lo1", 24, 48))
-    for b in range(4):
-        ts(a("j4", 3 * b, 3 * b + 3), a("lj", 0, 3), 2.0, ALU.mult, float(b), ALU.add)
-    gather("V", a("a0"), a("gt"), a("j4"), 0.5)
     gather("A", a("c4", 0, 384), a("o4"), a("lo1", 0, 24))
+    for b in range(4):
+        ts(a("j4", 3 * b, 3 * b + 3), a("lj", 0, 3), 4.0, ALU.mult, float(b), ALU.add)
+    gather("V", a("a0"), a("gt"), a("j4"), 0.5)
     gather("A", a("olt"), a("c4"), a("j4", 0, 3))
     for b in range(4):
         mm(b, "h", 128 * b, "l3", K, 128)

from concourse.mybir import dt, AluOpType, ActivationFunctionType

C, K = 192, 48
BF, F32, I32, U16, U8, X4 = "bfloat16", "float32", "int32", "uint16", "uint8", "float8_e4m3fn_x4"
SCRATCH = {"ps": ("psum", [128, 4096], F32)}
for _d, _names in (
        (X4, "wq:512 uq:128 urq:128 zq:144 vq:128 qq:144 eq:512 hq:512 f0q:512 f1q:512 b1q:384 bq:128 xq:128 "
             "l1q:192 l2q:192 l3q:176 r1q:96 r2q:96"),
        (U8, "wp:512 up:128 urp:128 zp:144 vp:128 qp:144 ep:512 hp:512 f0p:512 f1p:512 b1p:384 bp:128 xp:128 "
             "l1p:192 l2p:192 l3p:176 r1p:192 r2p:192"),
        (BF, "xt:1024 ut:512 zt:576 vt:512 qt:192 qx:576 f0:1024 t1:1024 f1:1024 t2:1024 hs:768 b1:512 bt:512 xo:512 gt:768 "
             "a0:192 et:515 ht:515 zero:576 ir:192 ip:192 jv:192 neg:192 one:16 m3:576 m4:192 c16:96 c16a:96 hm:96 "
             "i0:580 i1:580 ex3:576 ex4:192 o0:192 o1:192 eb:96 eg:96 nb:192 ob:192 junk:576 "
             "fz:576 fo:576 gz:576 hn:579 dj:579 us:579 far:4 o4:768 c4:768 m2:15 rm2:15 lm2:15"),
        (F32, "xf:192 q64:192 yt:48 olt:48 olx:48 old:4 cf:8 cs:48 eh:96 s0:12 s1:12 yg:96 ye:96 "
              "u0:12 u1:12 u2:12 u3:12 uc:4 sm:4"),
        (I32, "ci:16 cj:8"),
        (U16, "offu:8 p0:12 p1:12 g0:48 g1:48 so:6 m1:18 j2:4 j4:12 lm1:18 lo1:48 lj:4 rm1:18 ro1:48")):
    for _e in _names.split():
        SCRATCH[_e.split(":")[0]] = ("sbuf", [128, int(_e.split(":")[1])], _d)
SEMAPHORES = ["nV", "nA", "nP", "nG", "dx", "du", "dq", "dz", "dz2", "dv", "dwq", "dwp", "st", "ls",
              "a1", "a2", "a3", "am1", "am2", "ao", "aj", "h1", "h2", "hm1", "hm2", "ho"]
ALU, ACT = AluOpType, ActivationFunctionType
H = C // 2
PAD = 128 - H


def _mask(engines):
    m = 0
    for e in engines:
        m |= 1 << e
    return m


def _helpers(topo, src, dst):
    h = [c for c in topo.cores_of(src) if c != src and topo.may_write(c, dst)]
    near, far = [c for c in h if topo.die(c) == topo.die(src)], [c for c in h if topo.die(c) != topo.die(src)]
    return [far[0], near[0], near[1], far[1]]


def _hand_on(g, core, T, topo):
    n = len(T.cores)
    mine = [r for r in range(n) if T.cores[r] in topo.cores_of(core)]
    if not mine:
        return
    src, nxt, prv = T.cores[mine[0]], T.cores[(mine[0] + 1) % n], T.cores[(mine[0] - 1) % n]
    hs = _helpers(topo, src, nxt)
    full = len(topo.engines(src, core))
    sent = [0]

    def on(wait, cnt, out, in_, sem, dst):
        g.wait_ge(T.sem[wait], cnt)
        rid, pid = topo.addr(dst, core)
        g.remote_dma(out, in_, T.sem[sem], T.sem.ls, pid, rid, topo.mask(core, dst))
        sent[0] += len(topo.engines(core, dst))

    for s in "12":
        if core in hs[:2]:
            i = hs.index(core)
            on("h" + s, full, T["l%sq" % s][:, H * i:H * i + H].bitcast(dt.uint8),
               T["r%sq" % s][:].bitcast(dt.uint8), "a" + s, nxt)
        if core == hs[2]:
            on("h" + s, full, T["l%sp" % s][:], T["r%sp" % s][:], "a" + s, nxt)
            on("hm" + s, full, T["lm" + s][:], T["rm" + s][:], "am" + s, nxt)
    if core == _helpers(topo, src, prv)[3]:
        on("ho", full, T.lo1[:], T.ro1[:], "ao", prv)
    if sent[0]:
        g.wait_ge(T.sem.ls, sent[0])


def rank_program(g, core, T, topo):
    rank = T.rank_of(core)
    if rank is None:
        _hand_on(g, core, T, topo)
        return
    n = len(T.cores)
    nxt, prv, prv2, nxt2 = (T.cores[(rank + d) % n] for d in (1, -1, -2, 2))
    Q = {"V": g.vector, "A": g.scalar, "P": g.tensor, "G": g, "S": g.sync}
    known = {q: {} for q in Q}
    clock, acc, count = {}, {}, {}

    def a(name, lo=0, hi=None, step=1):
        hi = SCRATCH[name][1][1] if hi is None else hi
        cols = range(lo, hi, step)
        if name == "ps":
            cols = range(lo // 512 * 512, lo // 512 * 512 + 512)
        return (T[name][:, lo:hi:step] if step != 1 else T[name][:, lo:hi], name, frozenset(cols))

    def backwards(name, lo, hi, step=1):
        last = lo + (hi - 1 - lo) // step * step
        return (T[name][:, last:(lo - 1 if lo else None):-step], name, frozenset(range(lo, hi, step)))

    def need(q, tok):
        s, v = tok
        if known[q].get(s, 0) >= v:
            return
        Q[q].wait_ge(T.sem[s], v)
        for s2, v2 in clock.get(tok, {}).items():
            known[q][s2] = max(known[q].get(s2, 0), v2)
        known[q][s] = v

    def order(q, reads, writes):
        toks = {}
        for lst, wr in ((reads, False), (writes, True)):
            for _, name, cols in lst:
                for tq, tok, c2, w2 in acc.get(name, []):
                    if q == "P" and tq == "P":
                        continue
                    if (wr or w2 or (name == "ps" and tq != q)) and cols & c2:
                        toks[tok[0]] = max(toks.get(tok[0], 0), tok[1])
        for s in sorted(toks, key=lambda s: s == "n" + q):
            need(q, (s, toks[s]))

    def note(q, tok, reads, writes):
        clock[tok] = dict(known[q])
        for lst, wr in ((reads, False), (writes, True)):
            for _, name, cols in lst:
                acc.setdefault(name, []).append((q, tok, cols, wr))

    def op(q, fn, reads, writes):
        order(q, reads, writes)
        s = "n" + q
        fn().then_inc(T.sem[s], 1)
        count[s] = count.get(s, 0) + 1
        note(q, (s, count[s]), reads, writes)

    def lands(sem, cnt, *writes):
        count[sem] = cnt
        note("S", (sem, cnt), [], writes)

    def load(q, sem, out, src, w):
        Q[q].dma_start(out, src).then_inc(T.sem[sem], 16)
        count[sem] = 16
        note(q, (sem, 16), [], [w])

    def store(q, out, src, r):
        order(q, [r], [])
        Q[q].dma_start(out, src).then_inc(T.sem.st, 16)
        count["st"] = count.get("st", 0) + 16

    def send(d, sem, eng, out, in_, r):
        order("G", [r], [])
        rid, pid = topo.addr(d, core)
        g.remote_dma(out, in_, T.sem[sem], T.sem.ls, pid, rid, _mask(eng))
        count["ls"] = count.get("ls", 0) + len(eng)

    def sc(x):
        return (x[0], [x]) if isinstance(x, tuple) else (x, [])

    def ts(out, in0, s1, op0, s2=None, op1=None, off=None):
        (v1, r1), (v2, r2) = sc(s1), sc(s2)
        src = in0[0] if off is None else in0[0].indirect(off[0])
        args = (out[0], src, v1, v2, op0) + (() if op1 is None else (op1,))
        op("V", lambda: g.vector.tensor_scalar(*args), [in0] + r1 + r2 + ([off] if off else []), [out])

    def tt(out, in0, in1, o):
        op("V", lambda: g.vector.tensor_tensor(out[0], in0[0], in1[0], o), [in0, in1], [out])

    def scan(out, d0, d1, init, op0, op1):
        v, r = sc(init)
        op("V", lambda: g.vector.tensor_tensor_scan(out[0], d0[0], d1[0], v, op0, op1), [d0, d1] + r, [out])

    def fill(out, v):
        op("V", lambda: g.vector.memset(out[0], v), [], [out])

    def copy(out, in_):
        op("V", lambda: g.vector.tensor_copy(out[0], in_[0]), [in_], [out])

    def gather(q, out, win, off, scale=None, bias=None):
        if bias is not None:
            op("A", lambda: g.scalar.activation(out[0], win[0].indirect(off[0]), ACT.Identity, bias=bias), [win, off], [out])
        elif q == "A":
            kw = {} if scale is None else {"scale": scale}
            op("A", lambda: g.scalar.activation(out[0], win[0].indirect(off[0]), ACT.Copy, **kw), [win, off], [out])
        elif scale is None:
            op("V", lambda: g.vector.tensor_copy(out[0], win[0].indirect(off[0])), [win, off], [out])
        else:
            ts(out, win, scale, ALU.mult, off=off)

    def scaled(q, out, in_, s):
        if q == "A":
            op("A", lambda: g.scalar.activation(out[0], in_[0], ACT.Copy, scale=s), [in_], [out])
        else:
            ts(out, in_, s, ALU.mult)

    def zeros(name, lo, hi):
        scaled("A", a(name, lo, hi), a("zero", 0, hi - lo), 1.0)

    def pads(name):
        zeros(name, 0, 4 * PAD)
        zeros(name, 4 * (PAD + C), 1024)

    def quant(nm, lo, w, tile):
        c, p = a(nm + "q", lo, lo + w), a(nm + "p", lo, lo + w)
        op("V", lambda: g.vector.quantize_mx(c[0], p[0], tile[0]), [tile], [c, p])

    def pick(dst, src, w, off):
        c, p, c0, p0 = a(dst + "q", 0, w), a(dst + "p", 0, w), a(src + "q"), a(src + "p")
        op("V", lambda: g.vector.tensor_copy(c[0].bitcast(dt.uint32), c0[0].bitcast(dt.uint32).indirect(off[0])), [c0, off], [c])
        op("A", lambda: g.scalar.activation(p[0], p0[0].indirect(off[0]), ACT.Copy), [p0, off], [p])

    def mm(bank, st, slo, mv, mlo, w, start=True, stop=True):
        o = a("ps", 512 * bank, 512 * bank + w)
        r = [a(st + "q", slo, slo + 128), a(st + "p", slo, slo + 128), a(mv + "q", mlo, mlo + w), a(mv + "p", mlo, mlo + w)]
        op("P", lambda: g.tensor.matmul_mx(o[0], r[0][0], r[1][0], r[2][0], r[3][0], start, stop), r, [o])

    def bank(b, lo, hi):
        return a("ps", 512 * b + lo, 512 * b + hi)

    def iota(out, pattern, base, cm, small):
        kw = {"allow_small_or_imprecise_dtypes": True} if small else {}
        op("G", lambda: g.iota(out[0], pattern, base, cm, **kw), [], [out])

    hs = _helpers(topo, core, nxt)
    back = _helpers(topo, core, prv)[3]
    near = topo.engines(core, hs[0])

    def send_half(nm, s, i):
        r = a(nm + "q", PAD + H * i, PAD + H * i + H)
        send(hs[i], "h" + s, near, T["r%sq" % s][:].bitcast(dt.uint8), r[0].bitcast(dt.uint8), r)

    def send_scales(nm, s):
        p = a(nm + "p", PAD, PAD + C)
        send(hs[2], "h" + s, near, T["r%sp" % s][:], p[0], p)

    def via(src, i):
        return len(topo.engines(_helpers(topo, src, core)[i], core))

    direct = topo.engines(core, prv2)
    lands("a1", sum(via(prv, i) for i in range(3)), a("l1q"), a("l1p"))
    lands("a2", sum(via(prv, i) for i in range(3)), a("l2q"), a("l2p"))
    lands("a3", 2 * len(topo.engines(nxt2, core)), a("l3q", 128, 176), a("l3p", 128, 176))
    lands("am1", via(prv, 2), a("lm1"))
    lands("am2", via(prv, 2), a("lm2"))
    lands("ao", via(nxt, 3), a("lo1"))
    lands("aj", len(topo.engines(nxt2, core)), a("lj"))

    load("S", "du", T.ut[:], T.u[:], a("ut"))
    load("S", "dx", T.xt[:, 0:4 * C], T.x[:], a("xt", 0, 4 * C))
    need("S", ("dx", 16))
    load("S", "dq", T.qt[:], T.q[:], a("qt"))
    load("S", "dz", T.zt[:, 0:512], T.z[:], a("zt", 0, 512))
    load("S", "dz2", T.zt[:, 512:576], T.z[:, 0:64], a("zt", 512, 576))
    load("S", "dwq", T.wq[:].bitcast(dt.uint8), T.wc[:], a("wq"))
    load("S", "dwp", T.wp[:], T.ws[:], a("wp"))
    load("S", "dv", T.vt[:], T.v[:], a("vt"))

    pm, sel, q4 = (a("cf", i, i + 1) for i in range(3))
    sc3, sc4 = a("cs", 31, 32), a("cs", 39, 40)
    iota(a("ci", 0, 1), [[0, 1]], 0, 1, False)
    iota(a("ci", 8, 16), [[16, 8]], 0, 0, False)
    iota(a("ir"), [[0, 12], [1, 16]], 0, 0, True)
    fill(a("zero"), 0.0)
    ts(a("cj", 0, 1), a("ci", 0, 1), 15, ALU.bitwise_and)
    ts(a("cj", 1, 2), a("ci", 0, 1), 15, ALU.bitwise_and, 2, ALU.arith_shift_right)
    ts(a("cj", 2, 3), a("ci", 0, 1), 3, ALU.bitwise_and)
    fill(a("hm"), 0.5)
    copy(a("offu"), a("ci", 8, 16))
    copy(a("cf", 0, 2), a("cj", 0, 2))
    fill(a("neg"), -1.0)
    fill(a("one"), 1.0)
    ts(q4, a("cj", 2, 3), -4.0, ALU.add)
    fill(a("hm", 0, 96, 32), 0.0)
    fill(a("hm", 6, 96, 32), 0.0)
    iota(a("ip"), [[0, 48], [1, 4]], 0, 0, True)
    iota(a("jv"), [[4, C]], 4, 0, True)

    def diagonal(name, v):
        op("G", lambda: g.affine_select(T[name][:], T.zero[:, 0:515], [[-1, 515]], ALU.not_equal, v, 3, 4), [a("zero")], [a(name)])

    diagonal("et", 64.0)
    zeros("xt", 4 * C, 1024)
    zeros("o0", 0, C)
    pads("f0")

    def scores(b, nm, lo, t):
        for h in range(2):
            quant(nm, lo + 128 * h, 128, a(t, 512 * h, 512 * h + 512))
            mm(b + h, "ur", 0, nm, lo + 128 * h, 128)

    def bits(b, h, nm, lo, step, cmp, factor):
        w = (128, C - 128)[h]
        ts(a(nm, lo + 128 * h * step, lo + (128 * h + w) * step, step), bank(b + h, 0, w), 0.0, cmp, factor, ALU.mult)

    def gap(spare):
        if spare:
            for call in spare.pop(0):
                call()

    def sort(lv, b, t, spare):
        i, p, o, gl, f, to = "i%d" % lv, a("p%d" % lv), a("o%d" % lv), "g%d" % lv, "f%d" % lv, str(lv + 1)
        for h in range(2):
            bits(b, h, i, 4, 3, ALU.is_le, -1.0)
        gap(spare)
        scan(a(i, 3, 579, 3), a(i, 4, 580, 3), a("neg"), 256.0, ALU.add, ALU.max)
        scan(backwards(i, 5, 580, 3), backwards(i, 4, 580, 3), a("neg"), 255.0 - C, ALU.add, ALU.subtract)
        gap(spare)
        scan(a("ex3"), a("m3"), a(i, 3, 579), 0.0, ALU.mult, ALU.max)
        gap(spare)
        ts(p, a("ex3", 47, 576, 48), sc3, ALU.mult, 255.0, ALU.add)
        gap(spare)
        op("V", lambda: g.vector.tensor_copy(o[0].indirect(p[0]), T.jv[:]), [p, a("jv")], [o])
        gap(spare)
        scan(a("ex4"), a("m4"), o, 0.0, ALU.mult, ALU.max)
        gap(spare)
        ts(a(gl), a("ex4", 3, C, 4), sc4, ALU.mult, q4, ALU.add)
        if lv:
            send(back, "ho", near, T.ro1[:], T.g1[:], a("g1"))
        gap(spare)

        def part(q, lo, hi):
            gather(q, a(f, 4 * PAD + 16 * lo, 4 * PAD + 16 * hi), a(t, 0, 4 * C), a(gl, lo, hi))

        part("A", 12, 24)
        part("V", 0, 12)
        part("A", 32, 48)
        gap(spare)
        quant(f, 0, 128, a(f, 0, 512))
        send_half(f, to, 0)
        part("V", 24, 32)
        gap(spare)
        quant(f, 128, 128, a(f, 512, 1024))
        send_half(f, to, 1)
        send_scales(f, to)

    def step(lv, st, off, msg):
        i, ye = "i%d" % lv, a("ye", 15, 96, 16)
        if lv:
            last = [[lambda: ts(a(msg, 0, 6), a("u3", 0, 6), 4.0, ALU.mult, 4.0, ALU.add),
                     lambda: tt(a(msg, 9, 12), a("u3", 6, 9), a("u3", 3, 6), ALU.subtract),
                     lambda: ts(a(msg, 12, 15), a("u3", 3, 6), -256.0, ALU.mult, 256.0, ALU.add)] +
                    [lambda s=s: ts(a(msg, 6 + s, 7 + s), a("u3", 6 + s, 7 + s), a("u3", s, s + 1), ALU.subtract, 1.0, ALU.add)
                     for s in range(3)]]
        else:
            last = [[lambda: tt(a("u3", 9, 12), a("u3", 6, 9), a("u3", 0, 3), ALU.subtract),
                     lambda: ts(a(msg, 0, 6), a("u3", 0, 6), 3.0, ALU.mult)],
                    [lambda: copy(a(msg, 6, 18), a("u3", 0, 12))]]
        last[-1].append(lambda: send(hs[2], "h" + msg, near, T["r" + msg][:], T[msg][:], a(msg)))
        return [
            [lambda: gather("A", a("yg"), a(i, 0, 579), off, bias=1024.0),
             lambda: ts(a("uc", 3, 4), a(i, 576, 577), -1.0, ALU.mult, 256.0, ALU.add)],
            [lambda: scan(a("ye"), a("yg"), a("c16"), 0.0, ALU.max, ALU.add)],
            [lambda: tt(a("u0", 9, 12), a("ye", 15, 48, 16), a(st, 9, 12), ALU.subtract),
             lambda: tt(a("u1", 0, 6), a(st, 0, 6), ye, ALU.add),
             lambda: tt(a("u1", 6, 9), a(st, 6, 9), a("ye", 63, 96, 16), ALU.add)],
            [lambda: ts(a("u0", 0, 6), ye, -1.0, ALU.mult, 256.0, ALU.add),
             lambda: tt(a("uc", 0, 3), a("u0", 9, 12), a("ye", 63, 96, 16), ALU.is_le),
             lambda: ts(a("u0", 6, 9), a("u0", 9, 12), -1.0, ALU.mult, 256.0, ALU.add)],
            [lambda s=s: ts(a("u2", s, 9, 3), a("u1", s, 9, 3), a("uc", 3, 4), ALU.add, a("uc", s, s + 1), ALU.mult)
             for s in range(3)],
            [lambda: tt(a("u3", 0, 9), a("u0", 0, 9), a("u2", 0, 9), ALU.max)]] + last

    def layer(land, t, spare):
        for b in range(4):
            mm(b, "w", 128 * b, land, 0, C, True, False)
            mm(b, "e", 128 * b, land, 0, C, False, True)
            if b < 3:
                scaled("A", a(t, b, 4 * C, 4), bank(b, 0, C), 0.015625)
        gap([spare])
        scaled("V", a(t, 3, 512, 4), bank(3, 0, 128), 0.015625)
        scaled("V", a(t, 515, 4 * C, 4), bank(3, 128, C), 0.015625)

    def unit(nm):
        return [[lambda b=b: quant(nm, 128 * b, 128, a(nm + "t", 3 - b, 515 - b))] for b in range(4)]

    def query_scores():
        quant("q", 0, 144, a("qx"))
        mm(6, "z", 0, "q", 16, 128, True, False)
        mm(6, "z", 16, "q", 0, 128, False, True)

    quant("u", 0, 128, a("ut"))
    ts(a("m3", 0, 576, 3), a("ir"), pm, ALU.is_gt, 4.0, ALU.mult)
    pick("ur", "u", 128, a("offu"))
    ts(a("cs", 0, 16), a("m3", 0, 48, 3), -0.1875, ALU.mult, 1.0, ALU.add)
    scores(4, "f0", 256, "xt")
    zeros("qx", 0, 576)
    zeros("o1", 0, C)
    pads("f1")
    for t in ("t1", "t2"):
        zeros(t, 4 * C, 1024)
    zeros("b1", C, 512)
    for c in range(3):
        scaled("A", a("qx", 64 + 128 * c, 128 + 128 * c), a("qt", 64 * c, 64 * c + 64), 1.0)
    ts(a("m3", 1, 576, 3), a("m3", 0, 576, 3), 257.0 / 1024, ALU.mult, -1.0 / 256, ALU.add)
    ts(a("m3", 2, 576, 3), a("m3", 0, 576, 3), 64.25, ALU.mult, -256.0, ALU.add)
    ts(a("m4"), a("ip"), sel, ALU.is_gt, 256.0, ALU.mult)
    sort(0, 4, "xt", [
        [lambda: scan(a("cs", 16, 32), a("cs", 0, 16), a("one", 0, 16), -1.0, ALU.mult, ALU.mult)],
        [lambda: ts(a("cs", 32, 36), a("m4", 0, 4), -255.0 / 65536, ALU.mult, 1.0, ALU.add)],
        [lambda: scan(a("cs", 36, 40), a("cs", 32, 36), a("one", 0, 4), 1.0, ALU.mult, ALU.mult)],
        [lambda: ts(a("c16a"), a("ir", 0, 96), pm, ALU.is_lt, -4096.0, ALU.mult)],
        [lambda: quant("z", 0, 144, a("zt"))],
        [query_scores],
        [lambda: ts(a("c16"), a("ir", 0, 96), pm, ALU.is_equal, 4096.0, ALU.mult)],
        [lambda: ts(a("eb"), bank(6, 0, 96), 0.0, ALU.is_gt)],
        [lambda: op("V", lambda: g.vector.transpose(T.eg[:], T.eb[:]), [a("eb")], [a("eg")])]])

    first, e = step(0, "s0", a("so"), "m1"), unit("e")
    lo, k = a("eh", 5, 96, 32), a("eh", 12, 96, 32)
    scan(a("eh"), a("hm"), a("eg"), 0.0, ALU.mult, ALU.add)
    tt(a("c16"), a("c16"), a("c16a"), ALU.add)
    ts(a("so", 0, 3), lo, 96.0, ALU.mult)
    ts(a("so", 3, 6), lo, 96.0, ALU.mult, 384.0, ALU.add)
    fill(a("i0", 0, 3), 256.0)
    gap(first)
    ts(a("c16", 15, 96, 16), a("c16", 15, 96, 16), -5120.0, ALU.add)
    ts(a("s0", 0, 3), lo, 32.0, ALU.mult, -256.0, ALU.add)
    ts(a("s0", 9, 12), k, 64.0, ALU.mult)
    ts(a("s0", 3, 6), lo, 32.0, ALU.mult, -128.0, ALU.add)
    gap(e)
    tt(a("s0", 6, 9), a("s0", 0, 3), a("s0", 9, 12), ALU.add)
    zeros("o4", 0, 384)
    zeros("o4", 384, 768)
    for t in ("bt", "xo"):
        zeros(t, C, 512)
    scaled("A", a("q64"), a("qt", 0, C), 64.0)
    e += [[lambda: quant("l3", 0, 128, a("zero", 0, 512))], [lambda: quant("v", 0, 128, a("vt"))],
          [lambda: fill(a("hn", 0, 579, C + 1), -512.0), lambda: fill(a("j2"), 0), lambda: fill(a("i1", 0, 3), 256.0)]]
    while first or e:
        gap(first)
        gap(e)
    diagonal("ht", 0.5)
    iota(a("dj"), [[0, 3], [-1, C + 1]], C - 1, 0, True)

    layer("l1", "t1", [])
    scores(4, "f1", 256, "t1")
    second = step(1, "s1", a("lm1", 0, 6), "m2")
    pick_y, all_zeros = second.pop(0)
    calls = [call for group in second[1:4] for call in group]
    sort(1, 4, "t1", [
        [lambda: ts(a("s1", 0, 9), a("lm1", 6, 15), -256.0, ALU.add)],
        [pick_y, lambda: copy(a("s1", 9, 12), a("lm1", 15, 18))],
        [all_zeros], second[0]] + [calls[i:i + 2] for i in range(0, 9, 2)])

    for group in second[4:] + unit("h"):
        gap([group])
    for h in range(2):
        gather("A", a("gt", 384 * h, 384 * h + 384), a("f0", 4 * PAD, 4 * (PAD + C)), a("lo1", 24 * h, 24 * h + 24))
    ts(a("o4", 0, 768, 4), a("o0"), 0.25, ALU.mult, -1.0, ALU.add)

    def hpart(q, b):
        scaled(q, a("hs", C * b, C * b + C), bank(4 + b, 0, C), 1.0)

    def col(i, s):
        return a("lm2", 3 * i + s, 3 * i + s + 1)

    def hold_ones(s):
        ts(a("fo", C * s, C * s + C), a("jv"), col(1, s), ALU.is_ge, col(3, s), ALU.mult)

    layer("l2", "t2", [
        lambda s=s: ts(a("fz", C * s, C * s + C), a("jv"), col(0, s), ALU.is_lt, col(2, s), ALU.mult) for s in range(3)])
    for b in range(2):
        mm(4 + b, "h", 128 * b, "l2", 0, C, True, False)
    scores(0, "b1", 128, "t2")
    hold_ones(0)
    hold_ones(1)
    for b in range(4):
        if b >= 2:
            mm(4 + b, "h", 128 * b, "l2", 0, C, True, False)
        mm(4 + b, "h", 128 * b, "b1", 128, C, False, True)
    for h in range(2):
        bits(0, h, "nb", 0, 1, ALU.is_le, -1.0)
        bits(0, h, "ob", 0, 1, ALU.is_gt, 1.0)
    hold_ones(2)
    hpart("A", 0)
    for s in range(3):
        scan(a("gz", C * s, C * s + C), a("nb"), a("fz", C * s, C * s + C), col(2, s), ALU.add, ALU.max)
    for s in range(3):
        scan(a("hn", (C + 1) * s + 1, (C + 1) * (s + 1)), backwards("ob", 0, C), backwards("fo", C * s, C * s + C), col(3, s),
             ALU.add, ALU.min)
    for s in range(3):
        o, x, ac = a("junk", C * s, C * s + C), a("gz", C * s, C * s + C), a("sm", s, s + 1)
        op("A", lambda o=o, x=x, ac=ac: g.scalar.activation(o[0], x[0], ACT.Sign, accum_out=ac[0]), [x], [o, ac])
    for s in range(3):
        o, x, bc = a("far", s, s + 1), a("sm", s, s + 1), col(4, s)
        op("A", lambda o=o, x=x, bc=bc: g.scalar.activation(o[0], x[0], ACT.Relu, bias=bc[0], scale=256.0), [x, bc], [o])
    scaled("V", a("hs", C, C + H), bank(5, 0, H), 1.0)
    scan(a("us"), a("hn"), a("dj"), 0.0, ALU.add, ALU.max)
    scaled("V", a("hs", C + H, 2 * C), bank(5, H, C), 1.0)
    hpart("A", 2)
    hpart("A", 3)
    for s in range(3):
        ts(a("j2", s, s + 1), a("sm", s, s + 1), a("far", s, s + 1), ALU.subtract, a("us", (C + 1) * s + C, (C + 1) * (s + 1)), ALU.max)
    send(prv2, "aj", direct, T.lj[:], T.j2[:], a("j2"))
    for b in range(4):
        gather("VVAA"[b], a("b1", b, C, 4), a("hs", C * b, C * b + C), a("j2", 0, 3))
    quant("b1", 0, 128, a("b1"))
    rc, rp = a("b1q", 0, K), a("b1p", 0, K)
    send(prv2, "a3", direct, T.l3q[:, 128:176].bitcast(dt.uint8), rc[0].bitcast(dt.uint8), rc)
    send(prv2, "a3", direct, T.l3p[:, 128:176], rp[0], rp)

    gather("A", a("c4", 384, 768), a("o4"), a("lo1", 24, 48))
    gather("A", a("c4", 0, 384), a("o4"), a("lo1", 0, 24))
    for b in range(4):
        ts(a("j4", 3 * b, 3 * b + 3), a("lj", 0, 3), 4.0, ALU.mult, float(b), ALU.add)
    gather("V", a("a0"), a("gt"), a("j4"), 0.5)
    gather("A", a("olt"), a("c4"), a("j4", 0, 3))
    for b in range(4):
        mm(b, "h", 128 * b, "l3", K, 128)
        tt(a("bt", b, C, 4), bank(b, 80, 128), a("a0", K * b, K * b + K), ALU.add)
    quant("b", 0, 128, a("bt"))
    for c in range(3):
        scan(a("olx", 16 * c, 16 * c + 16), a("olt", c, K, 3), a("c16", 0, 16), 0.0, ALU.max, ALU.add)
    for b in range(4):
        mm(4 + b, "w", 128 * b, "b", 0, 128)
        tt(a("xf", b, C, 4), bank(4 + b, 0, K), a("q64", b, C, 4), ALU.add)
        scaled("AAAV"[b], a("xo", b, C, 4), a("xf", b, C, 4), 0.015625)
        if b == 0:
            ts(a("old", 0, 3), a("olx", 15, K, 16), 1024.0, ALU.add)
            store("S", T.ol[:], T.old[:, 0:3], a("old", 0, 3))
    quant("x", 0, 128, a("xo"))
    mm(0, "v", 0, "x", 0, 128)
    store("A", T.oc[:], T.xq[:, 0:K].bitcast(dt.uint8), a("xq"))
    for k in range(4):
        store("SSSA"[k], T.osc[4 * k:4 * k + 4, :], T.xp[32 * k:32 * k + 4, 0:K], a("xp"))
    copy(a("yt"), bank(0, 0, K))
    store("A", T.y[:], T.yt[:], a("yt"))
    for s in sorted(count):
        need("G", (s, count[s]))
